import numpy as np
import ml_dtypes


def mxq(x, axis, fmt="e4m3"):
    dtype, down = {"e4m3": (ml_dtypes.float8_e4m3fn, 7), "e5m2": (ml_dtypes.float8_e5m2, 14)}[fmt]
    v = np.moveaxis(np.asarray(x, np.float32).astype(ml_dtypes.bfloat16).astype(np.float64), axis, -1)
    blocks = v.reshape(v.shape[:-1] + (-1, 32))
    amax = np.abs(blocks).max(-1, keepdims=True)
    byte = np.maximum(np.where(amax > 0, np.frexp(amax)[1] - 1 + 127, 0) - down, 1)
    scale = np.exp2(byte - 127.0)
    codes = (blocks / scale).astype(np.float32).astype(dtype).astype(np.float64)
    return np.moveaxis((codes * scale).reshape(v.shape), -1, axis)


WIDE = False


def mx_kscale(k):
    if not WIDE:
        return np.ones(k)
    levels = np.array([10, -10, 5, -5, 0])
    if k % 512:
        return np.exp2(np.random.permutation(np.resize(levels, k // 32))).repeat(32)
    a = np.empty((k // 512, 16))
    for p in range(k // 512):
        a[p, :8] = np.random.permutation(np.resize(levels, 8))
        for g in range(8):
            far = levels[np.abs(levels - a[p, g]) >= 10]
            a[p, g + 8] = far[np.random.randint(len(far))]
    return np.exp2(a.ravel()).repeat(32)


BF16 = ml_dtypes.bfloat16


def bf(x):
    return np.asarray(x, np.float32).astype(BF16)


def f64(x):
    return np.asarray(x).astype(np.float64)

def planes(Y):
    n, m = Y.shape
    b = f64(bf(Y)).reshape(n // 32, 32, m)
    amax = np.abs(b).max(1)
    byte = np.clip(np.where(amax > 0, np.frexp(amax)[1] - 1 + 127 - 7, 1), 1, 254)
    codes = (b * np.exp2(127.0 - byte)[:, None, :]).reshape(n, m).astype(np.float32).astype(ml_dtypes.float8_e4m3fn).view(np.uint8)
    words = codes.reshape(n // 512, 128, 4, m).transpose(0, 1, 3, 2)
    return np.ascontiguousarray(words), np.ascontiguousarray(byte.astype(np.uint8).reshape(n // 512, 16, m))


MACH, SENS, FAULT, CREW = 2048, 1024, 1024, 512

def setup_inputs():
    s = mx_kscale(SENS)
    t = mx_kscale(MACH)
    rn = np.random.randn
    readings = rn(MACH, SENS) * s[None, :]
    signatures = 2.0 * rn(SENS, FAULT) / np.sqrt(SENS) / s[:, None]
    exposure = np.exp(0.3 * rn(MACH)) * t
    efforts = rn(MACH, CREW) / np.sqrt(MACH) / t[:, None]
    plan = 1.6 + 0.2 * rn(CREW)
    minimum = 1.0 + 0.1 * rn(CREW)
    skills = np.exp(0.7 * rn(FAULT, 1)) * np.exp(0.2 * rn(FAULT, CREW))
    return {"readings": bf(readings), "signatures": bf(signatures), "exposure": bf(exposure),
            "efforts": bf(efforts), "plan": bf(plan), "minimum": bf(minimum), "skills": bf(skills)}

def reference(readings, signatures, exposure, efforts, plan, minimum, skills):
    z = mxq(f64(readings), 1, "e4m3") @ mxq(f64(signatures), 0, "e4m3")
    h = f64(exposure)[:, None] / (1.0 + np.exp(-z))
    hq = mxq(h, 0, "e4m3")
    d = hq.T @ mxq(f64(efforts), 0, "e4m3")
    hours = np.maximum(d + f64(plan)[None, :], f64(minimum)[None, :])
    y = hours * f64(skills)
    Y = y
    words, scales = planes(Y)
    return y, words, scales

@@ -1,0 +1,577 @@
+from contextlib import ExitStack
+
+import concourse.mybir as mybir
+from concourse.masks import make_identity
+
+MACH, SENS, FAULT, CREW = 2048, 1024, 1024, 512
+FLOPS = 2 * MACH * SENS * FAULT + 2 * FAULT * MACH * CREW
+
+F32 = mybir.dt.float32
+BF16 = mybir.dt.bfloat16
+U32 = mybir.dt.uint32
+I32 = mybir.dt.int32
+U8 = mybir.dt.uint8
+FP8X4 = mybir.dt.float8_e4m3fn_x4
+ACT = mybir.ActivationFunctionType
+ALU = mybir.AluOpType
+
+P = 128
+PACK = 4
+KP = P * PACK
+
+
+def tile_fleet_fault_hours_h3_kernel(
+    tc, readings, signatures, exposure, efforts, plan, minimum, skills, out_0, out_1, out_2
+):
+    nc = tc.nc
+    with ExitStack() as ctx:
+        keep = ctx.enter_context(tc.tile_pool(name="keep", bufs=1))
+        work = ctx.enter_context(tc.tile_pool(name="work", bufs=2))
+        psum = ctx.enter_context(tc.psum_pool(name="psum", bufs=1))
+        ctx.enter_context(tc.manual_schedule())
+
+        def kept(name, shape, dtype):
+            return keep.tile(shape, dtype, name=name, align_bytes=64)
+
+        ident = kept("ident", [P, P], F32)
+        warm = kept("warm", [P, 8], F32)
+        expo = kept("expo", [P, 4, PACK], BF16)
+        rows_bf = kept("rows_bf", [P, P], BF16)
+        rows_f32 = kept("rows_f32", [P, P], F32)
+        crew_cols = kept("crew_cols", [P, 8], F32)
+        plan_less_min = kept("plan_less_min", [P, 4], F32)
+        r_raw = [[kept("r_raw%d%d" % (g, a), [P, 2, SENS], BF16) for a in range(2)] for g in range(4)]
+        r_codes = [kept("r_codes%d" % g, [P, PACK, 2, P], U32) for g in range(4)]
+        r_scales = [kept("r_scales%d" % g, [P, PACK, 2, P], U8) for g in range(4)]
+        s_raw = [[kept("s_raw%d%d" % (h, s), [P, PACK, KP], BF16) for s in range(2)] for h in range(2)]
+        s_codes = [kept("s_codes%d" % h, [P, 2, KP], U32) for h in range(2)]
+        s_scales = [kept("s_scales%d" % h, [P, 2, KP], U8) for h in range(2)]
+        e_raw = kept("e_raw", [P, 4, PACK, CREW], BF16)
+        e_codes = [kept("e_codes%d" % j, [P, 4, P], U32) for j in range(4)]
+        e_scales = [kept("e_scales%d" % j, [P, 4, P], U8) for j in range(4)]
+        h_codes = [kept("h_codes%d" % h, [P, 4, KP], U32) for h in range(2)]
+        h_scales = [kept("h_scales%d" % h, [P, 4, KP], U8) for h in range(2)]
+        skill = [kept("skill%d" % h, [P, PACK, CREW], BF16) for h in range(2)]
+        y = [kept("y%d" % h, [P, 4, PACK, P], F32) for h in range(2)]
+        y_bf = [kept("y_bf%d" % h, [P, CREW, PACK], BF16) for h in range(2)]
+        y_codes = [kept("y_codes%d" % h, [P, CREW], U32) for h in range(2)]
+        y_scales = [kept("y_scales%d" % h, [P, CREW], U8) for h in range(2)]
+        live = {}
+
+        def bank(b):
+            return psum.tile([P, KP], F32, name="bank%d" % b)
+
+        def grouped():
+            return work.tile([P, KP * PACK], BF16, name="grouped", bufs=5, align_bytes=64)
+
+        def copy_on(engine, out, in_):
+            if engine == "v":
+                nc.vector.tensor_copy(out=out, in_=in_)
+            else:
+                nc.scalar.copy(out=out, in_=in_)
+
+        def quantize(codes, scales, in_):
+            nc.vector.quantize_mx(out=codes.bitcast(FP8X4), scales=scales, in_=in_)
+
+        def load_readings(g, a):
+            rows = readings[KP * g : KP * (g + 1), :].rearrange("(p t) k -> p t k", t=PACK)
+            nc.sync.dma_start(out=r_raw[g][a][:], in_=rows[:, 2 * a : 2 * a + 2, :])
+
+        def load_signatures(h, s):
+            rows = signatures[KP * s : KP * (s + 1), KP * h : KP * (h + 1)]
+            nc.sync.dma_start(out=s_raw[h][s][:], in_=rows.rearrange("(p t) f -> p t f", t=PACK))
+
+        def load_efforts(g):
+            rows = efforts[KP * g : KP * (g + 1), :]
+            nc.sync.dma_start(out=e_raw[:, g, :, :], in_=rows.rearrange("(p t) c -> p t c", t=PACK))
+
+        def load_skills(h):
+            rows = skills[KP * h : KP * (h + 1), :]
+            nc.sync.dma_start(out=skill[h][:], in_=rows.rearrange("(p t) c -> p t c", t=PACK))
+
+        def T(g, t, b):
+            words = r_raw[g][t // 2][:, t % 2, :].bitcast(F32)
+            turned = bank(b)
+            live["T", g, t] = turned
+            for s in range(2):
+                for u in range(2):
+                    q = 2 * s + u
+                    nc.tensor.transpose(
+                        turned[:, P * q : P * (q + 1)], words[:, 256 * s + u : 256 * (s + 1) : 2], ident[:]
+                    )
+
+        def C(g, t, engine="s"):
+            if t % 2 == 0:
+                live["rg", g, t // 2] = grouped()
+            dst = live["rg", g, t // 2][:, 1024 * (t % 2) : 1024 * (t % 2 + 1)].bitcast(F32)
+            copy_on(
+                engine,
+                dst.rearrange("p (s r u) -> p s r u", s=2, u=2),
+                live["T", g, t][:].rearrange("p (s u r) -> p s r u", s=2, u=2),
+            )
+
+        def RQ(g, t0, t1):
+            src = live["rg", g, t0 // 2][:, 1024 * (t0 % 2) : 1024 * (t0 % 2 + t1 - t0)]
+            quantize(
+                r_codes[g][:, t0:t1, :, :].rearrange("p t s r -> p (t s r)"),
+                r_scales[g][:, t0:t1, :, :].rearrange("p t s r -> p (t s r)"),
+                src,
+            )
+
+        def SI(h, s, engine, c0=0, c1=KP):
+            if c0 == 0:
+                live["sg", h, s] = grouped()
+            dst = live["sg", h, s][:, PACK * c0 : PACK * c1]
+            copy_on(
+                engine,
+                dst.rearrange("p (c i t) -> p c t i", i=4, t=PACK),
+                s_raw[h][s][:, :, c0:c1].rearrange("p t (c i) -> p c t i", i=4),
+            )
+
+        def SQ(h, s):
+            quantize(s_codes[h][:, s, :], s_scales[h][:, s, :], live["sg", h, s][:])
+
+        def EI(j, engine, g0=0, g1=4):
+            if g0 == 0:
+                live["eg", j] = grouped()
+            dst = live["eg", j][:, KP * g0 : KP * g1]
+            copy_on(
+                engine,
+                dst.rearrange("p (g c i t) -> p g c t i", c=P // 4, i=4, t=PACK),
+                e_raw[:, g0:g1, :, P * j : P * (j + 1)].rearrange("p g t (c i) -> p g c t i", i=4),
+            )
+
+        def EQ(j):
+            quantize(
+                e_codes[j][:].rearrange("p g c -> p (g c)"),
+                e_scales[j][:].rearrange("p g c -> p (g c)"),
+                live["eg", j][:],
+            )
+
+        def Z(g, h, t, b):
+            z = bank(b)
+            live["z", g, h, t] = z
+            for s in range(2):
+                nc.tensor.matmul_mx(
+                    out=z[:],
+                    lhsT=r_codes[g][:, t, s, :].bitcast(FP8X4),
+                    lhsT_scale=r_scales[g][:, t, s, :],
+                    rhs=s_codes[h][:, s, :].bitcast(FP8X4),
+                    rhs_scale=s_scales[h][:, s, :],
+                    start=(s == 0),
+                    stop=(s == 1),
+                )
+
+        def S(g, h, t):
+            if t == 0:
+                live["sig", g, h] = work.tile([P, PACK, KP], F32, name="sig", bufs=3)
+            nc.scalar.activation(out=live["sig", g, h][:, t, :], in_=live["z", g, h, t][:], func=ACT.Sigmoid)
+
+        def M(g, h, c0=0, c1=KP):
+            if c0 == 0:
+                live["hg", g, h] = work.tile([P, KP * PACK], BF16, name="h_bf", bufs=2, align_bytes=64)
+            n = (c1 - c0) // 2
+            nc.vector.tensor_tensor(
+                out=live["hg", g, h][:, PACK * c0 : PACK * c1].rearrange("p (c i t) -> p c t i", i=2, t=PACK),
+                in0=live["sig", g, h][:, :, c0:c1].rearrange("p t (c i) -> p c t i", i=2),
+                in1=expo[:, g, :].unsqueeze(1).unsqueeze(3).broadcast_to([P, n, PACK, 2]),
+                op=ALU.mult,
+            )
+
+        def HQ(g, h, c0=0, c1=KP):
+            quantize(h_codes[h][:, g, c0:c1], h_scales[h][:, g, c0:c1], live["hg", g, h][:, PACK * c0 : PACK * c1])
+
+        def D(h, j, g0, g1, b=None):
+            if g0 == 0:
+                live["d", h, j] = bank(b)
+            for g in range(g0, g1):
+                nc.tensor.matmul_mx(
+                    out=live["d", h, j][:],
+                    lhsT=e_codes[j][:, g, :].bitcast(FP8X4),
+                    lhsT_scale=e_scales[j][:, g, :],
+                    rhs=h_codes[h][:, g, :].bitcast(FP8X4),
+                    rhs_scale=h_scales[h][:, g, :],
+                    start=(g == 0),
+                    stop=(g == 3),
+                )
+
+        def R(h, j, engine):
+            above = work.tile([P, PACK, P], F32, name="above", bufs=3)
+            live["r", h, j] = above
+            if engine == "v":
+                nc.vector.tensor_scalar(
+                    out=above[:],
+                    in0=live["d", h, j][:].rearrange("p (m t) -> p t m", t=PACK),
+                    scalar1=crew_cols[:, j : j + 1],
+                    scalar2=crew_cols[:, 4 + j : 5 + j],
+                    op0=ALU.add,
+                    op1=ALU.max,
+                )
+                return
+            nc.scalar.activation(
+                out=above[:],
+                in_=live["d", h, j][:].rearrange("p (m t) -> p t m", t=PACK),
+                func=ACT.Relu,
+                bias=plan_less_min[:, j : j + 1],
+            )
+            if engine == "s2":
+                nc.scalar.activation(
+                    out=above[:], in_=above[:], func=ACT.Identity, bias=crew_cols[:, 4 + j : 5 + j]
+                )
+
+        def UM(h, j, b, engine):
+            hours = bank(b)
+            live["u", h, j] = hours
+            live["fresh", h, j] = engine != "s"
+            if engine != "s":
+                return
+            for t in range(PACK):
+                nc.tensor.matmul(
+                    hours[:, P * t : P * (t + 1)],
+                    lhsT=crew_cols[:, 4 + j : 5 + j].to_broadcast([P, P]),
+                    rhs=ident[:],
+                    start=(t == 0),
+                    stop=False,
+                    is_transpose=True,
+                )
+
+        def U(h, j):
+            for t in range(PACK):
+                nc.tensor.matmul(
+                    live["u", h, j][:, P * t : P * (t + 1)],
+                    lhsT=live["r", h, j][:, t, :],
+                    rhs=ident[:],
+                    start=live["fresh", h, j],
+                    stop=(live["fresh", h, j] or t == PACK - 1),
+                    is_transpose=True,
+                )
+
+        def Y(h, j):
+            cols = slice(P * j, P * (j + 1))
+            nc.vector.tensor_tensor(
+                out=y[h][:, j, :, :],
+                in0=live["u", h, j][:].rearrange("p (t c) -> p t c", t=PACK),
+                in1=skill[h][:, :, cols],
+                op=ALU.mult,
+            )
+
+        def YB(h, j, engine):
+            copy_on(
+                engine,
+                y_bf[h][:, P * j : P * (j + 1), :].rearrange("p (c i) t -> p c t i", i=4),
+                y[h][:, j, :, :].rearrange("p t (c i) -> p c t i", i=4),
+            )
+
+        def YQ(h, j0, j1):
+            cols = slice(P * j0, P * j1)
+            quantize(y_codes[h][:, cols], y_scales[h][:, cols], y_bf[h][:, cols, :].rearrange("p c t -> p (c t)"))
+
+        def store_y(h, j):
+            cols = slice(P * j, P * (j + 1))
+            rows = out_0[KP * h : KP * (h + 1), :].rearrange("(p t) c -> p t c", t=PACK)
+            nc.sync.dma_start(out=rows[:, :, cols], in_=y[h][:, j, :, :])
+
+        def store_codes(h):
+            words = out_1[h].rearrange("p m t -> p (m t)").bitcast(I32)
+            nc.sync.dma_start(out=words, in_=y_codes[h][:].bitcast(I32))
+
+        def store_scales(h, quad, queue):
+            queue.dma_start(
+                out=out_2[h, 4 * quad : 4 * quad + 4, :].bitcast(I32),
+                in_=y_scales[h][32 * quad : 32 * quad + 4, :].bitcast(I32),
+            )
+
+        def setup():
+            nc.vector.memset(warm[:], 0.0)
+            nc.gpsimd.memset(rows_bf[:], 0.0)
+            make_identity(nc, ident[:])
+            nc.scalar.dma_start(out=expo[:], in_=exposure.rearrange("(g p t) -> p g t", p=P, t=PACK))
+            nc.scalar.dma_start(out=rows_bf[0:4, :], in_=plan.rearrange("(j c) -> j c", c=P))
+            nc.scalar.dma_start(out=rows_bf[4:8, :], in_=minimum.rearrange("(j c) -> j c", c=P))
+            nc.scalar.activation(out=warm[:, 4:5], in_=warm[:, 0:1], func=ACT.Sigmoid)
+
+        def rows_cast():
+            nc.scalar.copy(out=rows_f32[:], in_=rows_bf[:])
+
+        def rows_turn(b):
+            live["rows"] = bank(b)
+            nc.tensor.transpose(live["rows"][:, 0:P], rows_f32[:], ident[:])
+
+        def rows_out():
+            nc.vector.tensor_copy(out=crew_cols[:], in_=live["rows"][:, 0:8])
+
+        def rows_diff():
+            nc.vector.tensor_tensor(
+                out=plan_less_min[:], in0=crew_cols[:, 0:4], in1=crew_cols[:, 4:8], op=ALU.subtract
+            )
+
+        setup()
+        rows_cast()
+        load_readings(0,0)
+        load_signatures(0,0)
+        rows_turn(0)
+        T(0,0,1)
+        rows_out()
+        rows_diff()
+        C(0,0,"v")
+        load_readings(0,1)
+        load_signatures(0,1)
+        T(0,1,2)
+        load_readings(1,0)
+        load_signatures(1,0)
+        load_signatures(1,1)
+        SI(0,0,"v",0,256)
+        load_efforts(0)
+        RQ(0,0,1)
+        SI(0,0,"s",256,512)
+        T(0,2,3)
+        C(0,1,"s")
+        T(0,3,4)
+        T(1,0,5)
+        SQ(0,0)
+        load_efforts(1)
+        RQ(0,1,2)
+        C(0,2,"v")
+        SI(0,1,"v",0,256)
+        RQ(0,2,3)
+        SI(0,1,"s",256,512)
+        T(1,1,6)
+        load_efforts(2)
+        C(0,3,"s")
+        C(1,0,"s")
+        SI(1,0,"s",0,256)
+        SQ(0,1)
+        RQ(0,3,4)
+        Z(0,0,0,7)
+        load_readings(1,1)
+        SI(1,0,"v",256,512)
+        load_readings(2,0)
+        load_efforts(3)
+        Z(0,0,1,0)
+        Z(0,0,2,1)
+        C(1,1,"v")
+        SI(1,1,"v",0,256)
+        load_readings(2,1)
+        SI(1,1,"s",256,512)
+        RQ(1,0,2)
+        Z(0,0,3,2)
+        S(0,0,0)
+        Z(1,0,0,3)
+        S(0,0,1)
+        load_readings(3,0)
+        S(0,0,2)
+        S(0,0,3)
+        SQ(1,0)
+        SQ(1,1)
+        EI(0,"v",0,2)
+        Z(0,1,0,4)
+        EI(1,"s",0,2)
+        S(0,1,0)
+        Z(0,1,1,5)
+        T(1,2,6)
+        EI(2,"v",0,2)
+        T(1,3,7)
+        C(1,2,"s")
+        EI(3,"v",0,2)
+        S(0,1,1)
+        T(2,0,0)
+        Z(1,0,1,1)
+        C(1,3,"s")
+        M(0,0,0,256)
+        EI(1,"s",2,4)
+        Z(0,1,2,2)
+        M(0,0,256,512)
+        Z(0,1,3,4)
+        EI(0,"v",2,4)
+        S(0,1,2)
+        load_skills(0)
+        T(2,1,6)
+        S(1,0,0)
+        HQ(0,0)
+        T(2,2,5)
+        S(0,1,3)
+        load_readings(3,1)
+        EI(2,"v",2,4)
+        T(2,3,7)
+        EQ(0)
+        RQ(1,2,4)
+        T(3,0,2)
+        EQ(1)
+        C(2,2,"s")
+        C(2,0,"s")
+        Z(1,0,2,3)
+        EQ(2)
+        M(0,1,0,256)
+        Z(1,1,0,4)
+        S(1,0,1)
+        Z(1,0,3,5)
+        C(2,1,"s")
+        S(1,0,2)
+        M(0,1,256,512)
+        C(2,3,"s")
+        load_skills(1)
+        T(3,1,0)
+        S(1,0,3)
+        S(1,1,0)
+        T(3,2,1)
+        RQ(2,0,2)
+        C(3,0,"s")
+        T(3,3,6)
+        Z(1,1,1,3)
+        C(3,2,"s")
+        C(3,1,"s")
+        D(0,2,0,1,7)
+        HQ(0,1)
+        Z(1,1,2,5)
+        Z(1,1,3,4)
+        RQ(2,2,4)
+        S(1,1,1)
+        Z(2,0,0,2)
+        M(1,0,0,256)
+        Z(2,0,1,1)
+        S(1,1,2)
+        Z(2,1,0,0)
+        M(1,0,256,512)
+        S(1,1,3)
+        RQ(3,0,2)
+        D(0,0,0,1,3)
+        C(3,3,"s")
+        Z(2,0,2,5)
+        S(2,0,0)
+        S(2,0,1)
+        Z(2,0,3,4)
+        HQ(1,0)
+        M(1,1,0,256)
+        S(2,0,2)
+        Z(2,1,1,6)
+        Z(3,0,0,2)
+        D(0,0,1,2,None)
+        S(2,0,3)
+        M(1,1,256,512)
+        D(0,1,0,1,1)
+        D(0,2,1,2,None)
+        Z(3,0,1,5)
+        RQ(3,2,4)
+        S(2,1,0)
+        Z(3,0,2,4)
+        S(3,0,0)
+        Z(3,0,3,0)
+        S(2,1,1)
+        Z(2,1,2,2)
+        S(3,0,1)
+        M(2,0,0,256)
+        S(3,0,2)
+        M(2,0,256,512)
+        Z(2,1,3,6)
+        HQ(1,1)
+        Z(3,1,0,5)
+        HQ(2,0)
+        S(3,0,3)
+        S(2,1,2)
+        S(2,1,3)
+        D(1,0,0,1,4)
+        M(3,0,0,256)
+        Z(3,1,1,0)
+        EI(3,"s",2,4)
+        D(0,2,2,3,None)
+        S(3,1,0)
+        D(0,1,1,2,None)
+        D(0,0,2,3,None)
+        D(1,0,1,2,None)
+        S(3,1,1)
+        Z(3,1,2,2)
+        S(3,1,2)
+        D(0,1,2,3,None)
+        D(1,2,0,1,6)
+        M(3,0,256,512)
+        Z(3,1,3,5)
+        EQ(3)
+        D(1,3,0,1,0)
+        S(3,1,3)
+        HQ(3,0)
+        D(0,0,3,4,None)
+        D(1,1,0,1,2)
+        D(1,1,1,2,None)
+        D(0,1,3,4,None)
+        D(0,2,3,4,None)
+        D(1,2,1,2,None)
+        D(0,3,0,1,5)
+        D(0,3,1,2,None)
+        M(2,1,0,256)
+        M(2,1,256,512)
+        D(0,3,2,3,None)
+        M(3,1,0,256)
+        R(0,0,"s2")
+        UM(0,0,3,"s2")
+        D(0,3,3,4,None)
+        U(0,0)
+        D(1,3,1,2,None)
+        HQ(2,1)
+        M(3,1,256,512)
+        D(1,2,2,3,None)
+        R(0,1,"s2")
+        D(1,1,2,3,None)
+        UM(0,1,1,"s2")
+        D(1,0,2,3,None)
+        U(0,1)
+        R(0,2,"s2")
+        UM(0,2,7,"s2")
+        Y(0,0)
+        HQ(3,1)
+        U(0,2)
+        R(0,3,"s")
+        UM(0,3,3,"s")
+        U(0,3)
+        Y(0,1)
+        YB(0,0,"s")
+        Y(0,2)
+        store_y(0,0)
+        D(1,3,2,3,None)
+        D(1,0,3,4,None)
+        D(1,2,3,4,None)
+        YB(0,1,"s")
+        D(1,1,3,4,None)
+        R(1,0,"s")
+        D(1,3,3,4,None)
+        R(1,1,"s")
+        UM(1,0,5,"s")
+        store_y(0,1)
+        Y(0,3)
+        R(1,2,"s")
+        U(1,0)
+        YB(0,2,"v")
+        UM(1,1,1,"s")
+        YB(0,3,"v")
+        store_y(0,2)
+        R(1,3,"s")
+        YQ(0,0,4)
+        Y(1,0)
+        store_y(0,3)
+        U(1,1)
+        UM(1,2,7,"s")
+        Y(1,1)
+        U(1,2)
+        UM(1,3,3,"s")
+        store_codes(0)
+        YB(1,0,"s")
+        store_scales(0,0,nc.sync)
+        Y(1,2)
+        U(1,3)
+        YB(1,1,"s")
+        Y(1,3)
+        store_scales(0,1,nc.sync)
+        store_scales(0,2,nc.scalar)
+        YB(1,2,"v")
+        store_y(1,0)
+        store_scales(0,3,nc.sync)
+        store_y(1,1)
+        store_y(1,2)
+        YB(1,3,"v")
+        YQ(1,0,2)
+        store_y(1,3)
+        YQ(1,2,4)
+        store_codes(1)
+        store_scales(1,0,nc.sync)
+        store_scales(1,1,nc.sync)
+        store_scales(1,2,nc.scalar)
+        store_scales(1,3,nc.sync)

@@ -40,15 +40,15 @@ def tile_fleet_fault_hours_h3_kernel(
         rows_f32 = kept("rows_f32", [P, P], F32)
         crew_cols = kept("crew_cols", [P, 8], F32)
         plan_less_min = kept("plan_less_min", [P, 4], F32)
-        r_raw = [[kept("r_raw%d%d" % (g, a), [P, 2, SENS], BF16) for a in range(2)] for g in range(4)]
+        r_raw = [kept("r_raw%d" % g, [P, PACK, SENS], BF16) for g in range(4)]
         r_codes = [kept("r_codes%d" % g, [P, PACK, 2, P], U32) for g in range(4)]
         r_scales = [kept("r_scales%d" % g, [P, PACK, 2, P], U8) for g in range(4)]
         s_raw = [[kept("s_raw%d%d" % (h, s), [P, PACK, KP], BF16) for s in range(2)] for h in range(2)]
         s_codes = [kept("s_codes%d" % h, [P, 2, KP], U32) for h in range(2)]
         s_scales = [kept("s_scales%d" % h, [P, 2, KP], U8) for h in range(2)]
-        e_raw = kept("e_raw", [P, 4, PACK, CREW], BF16)
-        e_codes = [kept("e_codes%d" % j, [P, 4, P], U32) for j in range(4)]
-        e_scales = [kept("e_scales%d" % j, [P, 4, P], U8) for j in range(4)]
+        e_raw = [kept("e_raw%d" % g, [P, PACK, CREW], BF16) for g in range(4)]
+        e_codes = [kept("e_codes%d" % j, [P, CREW], U32) for j in range(4)]
+        e_scales = [kept("e_scales%d" % j, [P, CREW], U8) for j in range(4)]
         h_codes = [kept("h_codes%d" % h, [P, 4, KP], U32) for h in range(2)]
         h_scales = [kept("h_scales%d" % h, [P, 4, KP], U8) for h in range(2)]
         skill = [kept("skill%d" % h, [P, PACK, CREW], BF16) for h in range(2)]
@@ -73,9 +73,9 @@ def tile_fleet_fault_hours_h3_kernel(
         def quantize(codes, scales, in_):
             nc.vector.quantize_mx(out=codes.bitcast(FP8X4), scales=scales, in_=in_)
 
-        def load_readings(g, a):
+        def load_readings(g, t0, t1):
             rows = readings[KP * g : KP * (g + 1), :].rearrange("(p t) k -> p t k", t=PACK)
-            nc.sync.dma_start(out=r_raw[g][a][:], in_=rows[:, 2 * a : 2 * a + 2, :])
+            nc.sync.dma_start(out=r_raw[g][:, t0:t1, :], in_=rows[:, t0:t1, :])
 
         def load_signatures(h, s):
             rows = signatures[KP * s : KP * (s + 1), KP * h : KP * (h + 1)]
@@ -83,14 +83,14 @@ def tile_fleet_fault_hours_h3_kernel(
 
         def load_efforts(g):
             rows = efforts[KP * g : KP * (g + 1), :]
-            nc.sync.dma_start(out=e_raw[:, g, :, :], in_=rows.rearrange("(p t) c -> p t c", t=PACK))
+            nc.sync.dma_start(out=e_raw[g][:], in_=rows.rearrange("(p t) c -> p t c", t=PACK))
 
         def load_skills(h):
             rows = skills[KP * h : KP * (h + 1), :]
             nc.sync.dma_start(out=skill[h][:], in_=rows.rearrange("(p t) c -> p t c", t=PACK))
 
         def T(g, t, b):
-            words = r_raw[g][t // 2][:, t % 2, :].bitcast(F32)
+            words = r_raw[g][:, t, :].bitcast(F32)
             turned = bank(b)
             live["T", g, t] = turned
             for s in range(2):
@@ -131,22 +131,17 @@ def tile_fleet_fault_hours_h3_kernel(
         def SQ(h, s):
             quantize(s_codes[h][:, s, :], s_scales[h][:, s, :], live["sg", h, s][:])
 
-        def EI(j, engine, g0=0, g1=4):
-            if g0 == 0:
-                live["eg", j] = grouped()
-            dst = live["eg", j][:, KP * g0 : KP * g1]
+        def EI(g, a, engine, chained):
+            if a == 0:
+                live["eg", g] = grouped()
             copy_on(
                 engine,
-                dst.rearrange("p (g c i t) -> p g c t i", c=P // 4, i=4, t=PACK),
-                e_raw[:, g0:g1, :, P * j : P * (j + 1)].rearrange("p g t (c i) -> p g c t i", i=4),
+                live["eg", g][:, 1024 * a : 1024 * (a + 1)].rearrange("p (c i t) -> p c t i", i=4, t=PACK),
+                e_raw[g][:, :, 256 * a : 256 * (a + 1)].rearrange("p t (c i) -> p c t i", i=4),
             )
 
-        def EQ(j):
-            quantize(
-                e_codes[j][:].rearrange("p g c -> p (g c)"),
-                e_scales[j][:].rearrange("p g c -> p (g c)"),
-                live["eg", j][:],
-            )
+        def EQ(g, a0, a1):
+            quantize(e_codes[g][:], e_scales[g][:], live["eg", g][:])
 
         def Z(g, h, t, b):
             z = bank(b)
@@ -187,8 +182,8 @@ def tile_fleet_fault_hours_h3_kernel(
             for g in range(g0, g1):
                 nc.tensor.matmul_mx(
                     out=live["d", h, j][:],
-                    lhsT=e_codes[j][:, g, :].bitcast(FP8X4),
-                    lhsT_scale=e_scales[j][:, g, :],
+                    lhsT=e_codes[g][:, P * j : P * (j + 1)].bitcast(FP8X4),
+                    lhsT_scale=e_scales[g][:, P * j : P * (j + 1)],
                     rhs=h_codes[h][:, g, :].bitcast(FP8X4),
                     rhs_scale=h_scales[h][:, g, :],
                     start=(g == 0),
@@ -285,10 +280,14 @@ def tile_fleet_fault_hours_h3_kernel(
             nc.vector.memset(warm[:], 0.0)
             nc.gpsimd.memset(rows_bf[:], 0.0)
             make_identity(nc, ident[:])
-            nc.scalar.dma_start(out=expo[:], in_=exposure.rearrange("(g p t) -> p g t", p=P, t=PACK))
-            nc.scalar.dma_start(out=rows_bf[0:4, :], in_=plan.rearrange("(j c) -> j c", c=P))
-            nc.scalar.dma_start(out=rows_bf[4:8, :], in_=minimum.rearrange("(j c) -> j c", c=P))
             nc.scalar.activation(out=warm[:, 4:5], in_=warm[:, 0:1], func=ACT.Sigmoid)
+
+        def load_crew(which):
+            vec = (plan, minimum)[which]
+            nc.sync.dma_start(out=rows_bf[4 * which : 4 * which + 4, :], in_=vec.rearrange("(j c) -> j c", c=P))
+
+        def load_exposure():
+            nc.sync.dma_start(out=expo[:], in_=exposure.rearrange("(g p t) -> p g t", p=P, t=PACK))
 
         def rows_cast():
             nc.scalar.copy(out=rows_f32[:], in_=rows_bf[:])
@@ -306,272 +305,277 @@ def tile_fleet_fault_hours_h3_kernel(
             )
 
         setup()
-        rows_cast()
-        load_readings(0,0)
+        load_readings(0,0,1)
+        load_readings(0,1,2)
         load_signatures(0,0)
-        rows_turn(0)
-        T(0,0,1)
-        rows_out()
-        rows_diff()
-        C(0,0,"v")
-        load_readings(0,1)
-        load_signatures(0,1)
-        T(0,1,2)
-        load_readings(1,0)
-        load_signatures(1,0)
-        load_signatures(1,1)
+        T(0,0,0)
         SI(0,0,"v",0,256)
-        load_efforts(0)
-        RQ(0,0,1)
+        C(0,0,"v")
+        load_signatures(0,1)
         SI(0,0,"s",256,512)
-        T(0,2,3)
+        SI(0,1,"s",0,256)
+        load_readings(0,2,3)
+        SI(0,1,"v",256,512)
+        T(0,1,1)
+        load_readings(0,3,4)
+        load_signatures(1,0)
         C(0,1,"s")
-        T(0,3,4)
-        T(1,0,5)
         SQ(0,0)
-        load_efforts(1)
-        RQ(0,1,2)
-        C(0,2,"v")
-        SI(0,1,"v",0,256)
-        RQ(0,2,3)
-        SI(0,1,"s",256,512)
-        T(1,1,6)
-        load_efforts(2)
-        C(0,3,"s")
-        C(1,0,"s")
-        SI(1,0,"s",0,256)
+        T(0,2,2)
+        RQ(0,0,1)
+        T(0,3,3)
         SQ(0,1)
-        RQ(0,3,4)
-        Z(0,0,0,7)
-        load_readings(1,1)
+        Z(0,0,0,4)
+        load_signatures(1,1)
+        RQ(0,1,2)
+        load_readings(1,0,2)
+        C(0,2,"s")
+        SI(1,0,"s",0,256)
+        load_crew(1)
+        load_efforts(0)
+        Z(0,0,1,5)
+        RQ(0,2,3)
+        T(1,0,6)
+        T(1,1,7)
         SI(1,0,"v",256,512)
-        load_readings(2,0)
-        load_efforts(3)
-        Z(0,0,1,0)
-        Z(0,0,2,1)
-        C(1,1,"v")
-        SI(1,1,"v",0,256)
-        load_readings(2,1)
-        SI(1,1,"s",256,512)
-        RQ(1,0,2)
-        Z(0,0,3,2)
+        SI(1,1,"s",0,256)
+        load_crew(0)
+        load_efforts(1)
+        C(0,3,"s")
+        SI(1,1,"v",256,512)
         S(0,0,0)
-        Z(1,0,0,3)
-        S(0,0,1)
-        load_readings(3,0)
-        S(0,0,2)
-        S(0,0,3)
         SQ(1,0)
         SQ(1,1)
-        EI(0,"v",0,2)
-        Z(0,1,0,4)
-        EI(1,"s",0,2)
+        rows_cast()
+        C(1,0,"s")
+        Z(0,0,2,0)
+        RQ(0,3,4)
+        S(0,0,1)
+        Z(0,1,0,1)
+        EI(0,0,"v",False)
+        S(0,0,2)
+        load_efforts(2)
+        C(1,1,"s")
+        EI(0,1,"v",False)
+        EI(1,0,"v",False)
+        Z(0,1,1,2)
         S(0,1,0)
-        Z(0,1,1,5)
-        T(1,2,6)
-        EI(2,"v",0,2)
-        T(1,3,7)
-        C(1,2,"s")
-        EI(3,"v",0,2)
+        EQ(0,0,2)
+        EI(2,0,"v",False)
+        Z(0,0,3,3)
+        load_exposure()
+        load_readings(1,2,4)
+        load_readings(2,0,2)
+        load_readings(2,2,4)
+        Z(0,1,2,4)
         S(0,1,1)
-        T(2,0,0)
-        Z(1,0,1,1)
-        C(1,3,"s")
-        M(0,0,0,256)
-        EI(1,"s",2,4)
-        Z(0,1,2,2)
-        M(0,0,256,512)
-        Z(0,1,3,4)
-        EI(0,"v",2,4)
+        EI(1,1,"v",False)
         S(0,1,2)
-        load_skills(0)
-        T(2,1,6)
-        S(1,0,0)
-        HQ(0,0)
-        T(2,2,5)
+        Z(0,1,3,6)
+        RQ(1,0,2)
+        rows_turn(5)
+        T(1,2,0)
+        rows_out()
+        EQ(1,0,2)
+        T(1,3,7)
+        T(2,0,1)
+        S(0,0,3)
+        M(0,0,0,256)
+        load_readings(3,0,2)
+        C(1,2,"s")
+        T(2,1,2)
+        T(2,2,4)
+        T(2,3,5)
+        Z(1,1,0,3)
+        Z(1,0,0,0)
         S(0,1,3)
-        load_readings(3,1)
-        EI(2,"v",2,4)
-        T(2,3,7)
-        EQ(0)
-        RQ(1,2,4)
-        T(3,0,2)
-        EQ(1)
-        C(2,2,"s")
+        C(1,3,"s")
         C(2,0,"s")
-        Z(1,0,2,3)
-        EQ(2)
+        Z(1,1,1,6)
+        C(2,2,"s")
+        rows_diff()
+        EI(2,1,"s",False)
         M(0,1,0,256)
-        Z(1,1,0,4)
-        S(1,0,1)
-        Z(1,0,3,5)
+        Z(1,0,1,7)
+        RQ(1,2,4)
         C(2,1,"s")
-        S(1,0,2)
-        M(0,1,256,512)
+        Z(1,0,2,1)
+        M(0,0,256,512)
         C(2,3,"s")
-        load_skills(1)
-        T(3,1,0)
+        load_readings(3,2,4)
+        S(1,0,0)
+        M(0,1,256,512)
+        S(1,0,1)
+        Z(1,1,2,4)
+        S(1,0,2)
+        Z(1,0,3,2)
+        Z(1,1,3,5)
         S(1,0,3)
-        S(1,1,0)
-        T(3,2,1)
+        T(3,0,0)
         RQ(2,0,2)
+        T(3,1,7)
+        T(3,2,1)
+        S(1,1,0)
+        HQ(0,0)
+        T(3,3,2)
         C(3,0,"s")
-        T(3,3,6)
-        Z(1,1,1,3)
-        C(3,2,"s")
-        C(3,1,"s")
-        D(0,2,0,1,7)
-        HQ(0,1)
-        Z(1,1,2,5)
-        Z(1,1,3,4)
-        RQ(2,2,4)
         S(1,1,1)
-        Z(2,0,0,2)
-        M(1,0,0,256)
-        Z(2,0,1,1)
+        RQ(2,2,4)
+        EQ(2,0,2)
+        HQ(0,1)
         S(1,1,2)
-        Z(2,1,0,0)
-        M(1,0,256,512)
+        M(1,0,0,256)
+        D(0,1,0,1,3)
+        Z(2,0,0,0)
         S(1,1,3)
-        RQ(3,0,2)
-        D(0,0,0,1,3)
-        C(3,3,"s")
-        Z(2,0,2,5)
+        C(3,1,"s")
+        load_skills(0)
         S(2,0,0)
-        S(2,0,1)
-        Z(2,0,3,4)
-        HQ(1,0)
+        M(1,0,256,512)
         M(1,1,0,256)
+        C(3,2,"s")
+        RQ(3,0,2)
+        Z(2,0,1,6)
+        Z(2,1,0,4)
+        S(2,0,1)
+        Z(2,0,2,5)
+        D(0,3,0,1,7)
         S(2,0,2)
-        Z(2,1,1,6)
-        Z(3,0,0,2)
-        D(0,0,1,2,None)
+        Z(2,0,3,0)
+        C(3,3,"s")
         S(2,0,3)
+        Z(3,0,0,1)
+        Z(2,1,1,6)
+        D(0,2,0,1,5)
+        Z(3,0,1,2)
         M(1,1,256,512)
-        D(0,1,0,1,1)
-        D(0,2,1,2,None)
-        Z(3,0,1,5)
-        RQ(3,2,4)
         S(2,1,0)
-        Z(3,0,2,4)
-        S(3,0,0)
-        Z(3,0,3,0)
-        S(2,1,1)
-        Z(2,1,2,2)
-        S(3,0,1)
-        M(2,0,0,256)
-        S(3,0,2)
-        M(2,0,256,512)
-        Z(2,1,3,6)
-        HQ(1,1)
-        Z(3,1,0,5)
-        HQ(2,0)
-        S(3,0,3)
-        S(2,1,2)
-        S(2,1,3)
-        D(1,0,0,1,4)
-        M(3,0,0,256)
-        Z(3,1,1,0)
-        EI(3,"s",2,4)
-        D(0,2,2,3,None)
-        S(3,1,0)
-        D(0,1,1,2,None)
-        D(0,0,2,3,None)
-        D(1,0,1,2,None)
-        S(3,1,1)
-        Z(3,1,2,2)
-        S(3,1,2)
-        D(0,1,2,3,None)
-        D(1,2,0,1,6)
-        M(3,0,256,512)
-        Z(3,1,3,5)
-        EQ(3)
-        D(1,3,0,1,0)
-        S(3,1,3)
-        HQ(3,0)
-        D(0,0,3,4,None)
-        D(1,1,0,1,2)
-        D(1,1,1,2,None)
-        D(0,1,3,4,None)
-        D(0,2,3,4,None)
-        D(1,2,1,2,None)
-        D(0,3,0,1,5)
+        HQ(1,0)
         D(0,3,1,2,None)
-        M(2,1,0,256)
-        M(2,1,256,512)
+        D(0,1,1,2,None)
+        RQ(3,2,4)
+        S(3,0,0)
+        M(2,0,0,256)
+        M(2,0,256,512)
+        S(2,1,1)
+        S(3,0,1)
+        HQ(1,1)
+        D(0,0,0,1,0)
+        HQ(2,0)
+        load_efforts(3)
+        Z(3,0,2,4)
+        S(3,0,2)
+        Z(3,0,3,1)
+        S(3,0,3)
+        D(0,0,1,2,None)
+        M(3,0,0,256)
+        Z(2,1,2,6)
+        Z(2,1,3,2)
+        D(0,2,1,2,None)
+        EI(3,0,"s",False)
+        EI(3,1,"s",False)
+        S(2,1,2)
+        D(0,0,2,3,None)
+        S(2,1,3)
+        M(3,0,256,512)
+        EQ(3,0,2)
+        Z(3,1,0,4)
+        D(0,2,2,3,None)
         D(0,3,2,3,None)
+        S(3,1,0)
+        Z(3,1,1,1)
+        HQ(3,0)
+        M(2,1,0,256)
+        Z(3,1,2,6)
+        S(3,1,1)
+        Z(3,1,3,2)
+        D(1,1,0,1,4)
+        D(0,0,3,4,None)
+        D(0,2,3,4,None)
+        S(3,1,2)
+        M(2,1,256,512)
+        S(3,1,3)
+        D(1,0,0,1,1)
         M(3,1,0,256)
-        R(0,0,"s2")
-        UM(0,0,3,"s2")
+        D(1,2,0,1,6)
         D(0,3,3,4,None)
-        U(0,0)
-        D(1,3,1,2,None)
+        D(0,1,2,3,None)
+        D(0,1,3,4,None)
+        UM(0,0,2,"s2")
+        D(1,1,1,2,None)
         HQ(2,1)
         M(3,1,256,512)
-        D(1,2,2,3,None)
-        R(0,1,"s2")
-        D(1,1,2,3,None)
-        UM(0,1,1,"s2")
-        D(1,0,2,3,None)
-        U(0,1)
-        R(0,2,"s2")
-        UM(0,2,7,"s2")
+        D(1,2,1,2,None)
+        R(0,0,"s2")
+        D(1,0,1,2,None)
+        load_skills(1)
+        U(0,0)
+        UM(0,1,0,"s")
+        R(0,1,"s")
+        UM(0,2,3,"s")
         Y(0,0)
+        store_y(0,0)
+        R(0,2,"s")
+        U(0,1)
         HQ(3,1)
         U(0,2)
-        R(0,3,"s")
-        UM(0,3,3,"s")
-        U(0,3)
+        R(0,3,"s2")
         Y(0,1)
+        D(1,0,2,3,None)
         YB(0,0,"s")
+        D(1,3,0,1,5)
+        D(1,1,2,3,None)
+        UM(0,3,2,"s2")
+        U(0,3)
         Y(0,2)
-        store_y(0,0)
-        D(1,3,2,3,None)
         D(1,0,3,4,None)
-        D(1,2,3,4,None)
-        YB(0,1,"s")
-        D(1,1,3,4,None)
-        R(1,0,"s")
-        D(1,3,3,4,None)
-        R(1,1,"s")
-        UM(1,0,5,"s")
         store_y(0,1)
-        Y(0,3)
-        R(1,2,"s")
-        U(1,0)
-        YB(0,2,"v")
-        UM(1,1,1,"s")
-        YB(0,3,"v")
+        D(1,1,3,4,None)
+        D(1,3,1,2,None)
+        YB(0,1,"s")
+        D(1,3,2,3,None)
         store_y(0,2)
-        R(1,3,"s")
-        YQ(0,0,4)
-        Y(1,0)
+        Y(0,3)
+        D(1,2,2,3,None)
+        YB(0,2,"s")
+        R(1,0,"v")
+        UM(1,0,7,"v")
+        D(1,3,3,4,None)
+        D(1,2,3,4,None)
         store_y(0,3)
-        U(1,1)
-        UM(1,2,7,"s")
-        Y(1,1)
-        U(1,2)
-        UM(1,3,3,"s")
+        R(1,1,"s")
+        U(1,0)
+        YB(0,3,"v")
+        R(1,2,"s")
+        UM(1,1,0,"s")
+        YQ(0,0,4)
         store_codes(0)
-        YB(1,0,"s")
-        store_scales(0,0,nc.sync)
-        Y(1,2)
-        U(1,3)
-        YB(1,1,"s")
-        Y(1,3)
+        Y(1,0)
+        U(1,1)
+        store_scales(0,0,nc.scalar)
         store_scales(0,1,nc.sync)
-        store_scales(0,2,nc.scalar)
-        YB(1,2,"v")
-        store_y(1,0)
+        R(1,3,"s")
+        store_scales(0,2,nc.sync)
+        UM(1,2,3,"s")
+        YB(1,0,"s")
+        U(1,2)
         store_scales(0,3,nc.sync)
+        Y(1,1)
+        UM(1,3,2,"s")
+        Y(1,2)
+        store_y(1,0)
+        YB(1,1,"s")
+        U(1,3)
+        YB(1,2,"s")
         store_y(1,1)
         store_y(1,2)
-        YB(1,3,"v")
+        Y(1,3)
         YQ(1,0,2)
-        store_y(1,3)
+        YB(1,3,"v")
         YQ(1,2,4)
+        store_y(1,3)
+        store_scales(1,0,nc.scalar)
+        store_scales(1,1,nc.scalar)
         store_codes(1)
-        store_scales(1,0,nc.sync)
-        store_scales(1,1,nc.sync)
-        store_scales(1,2,nc.scalar)
-        store_scales(1,3,nc.sync)
+        store_scales(1,2,nc.sync)
+        store_scales(1,3,nc.scalar)

@@ -35,7 +35,10 @@ def tile_fleet_fault_hours_h3_kernel(
 
         ident = kept("ident", [P, P], F32)
         warm = kept("warm", [P, 8], F32)
-        expo = kept("expo", [P, 4, PACK], BF16)
+        expo_bf = kept("expo_bf", [P, KP], BF16)
+        expo_f32 = kept("expo_f32", [P, PACK, P], F32)
+        expo_sb = kept("expo_sb", [P, 4, PACK], F32)
+        expo = psum.tile([P, PACK, P], F32, name="expo")
         rows_bf = kept("rows_bf", [P, P], BF16)
         rows_f32 = kept("rows_f32", [P, P], F32)
         crew_cols = kept("crew_cols", [P, 8], F32)
@@ -162,14 +165,21 @@ def tile_fleet_fault_hours_h3_kernel(
                 live["sig", g, h] = work.tile([P, PACK, KP], F32, name="sig", bufs=3)
             nc.scalar.activation(out=live["sig", g, h][:, t, :], in_=live["z", g, h, t][:], func=ACT.Sigmoid)
 
-        def M(g, h, c0=0, c1=KP):
-            if c0 == 0:
-                live["hg", g, h] = work.tile([P, KP * PACK], BF16, name="h_bf", bufs=2, align_bytes=64)
-            n = (c1 - c0) // 2
+        def M(g, h):
+            h_bf = work.tile([P, KP * PACK], BF16, name="h_bf", bufs=1, align_bytes=64)
+            live["hg", g, h] = h_bf
+            sig = live["sig", g, h]
+            split = 384
+            nc.gpsimd.tensor_tensor(
+                out=h_bf[:, PACK * split :].rearrange("p (c t) -> p c t", t=PACK),
+                in0=sig[:, :, split:].rearrange("p t c -> p c t"),
+                in1=expo_sb[:, g : g + 1, :].broadcast_to([P, KP - split, PACK]),
+                op=ALU.mult,
+            )
             nc.vector.tensor_tensor(
-                out=live["hg", g, h][:, PACK * c0 : PACK * c1].rearrange("p (c i t) -> p c t i", i=2, t=PACK),
-                in0=live["sig", g, h][:, :, c0:c1].rearrange("p t (c i) -> p c t i", i=2),
-                in1=expo[:, g, :].unsqueeze(1).unsqueeze(3).broadcast_to([P, n, PACK, 2]),
+                out=h_bf[:, : PACK * split].rearrange("p (c i t) -> p c t i", i=2, t=PACK),
+                in0=sig[:, :, :split].rearrange("p t (c i) -> p c t i", i=2),
+                in1=expo[:, :, g : g + 1].unsqueeze(1).broadcast_to([P, split // 2, PACK, 2]),
                 op=ALU.mult,
             )
 
@@ -280,6 +290,7 @@ def tile_fleet_fault_hours_h3_kernel(
             nc.vector.memset(warm[:], 0.0)
             nc.gpsimd.memset(rows_bf[:], 0.0)
             make_identity(nc, ident[:])
+            nc.gpsimd.memset(expo_bf[:], 0.0)
             nc.scalar.activation(out=warm[:, 4:5], in_=warm[:, 0:1], func=ACT.Sigmoid)
 
         def load_crew(which):
@@ -287,7 +298,17 @@ def tile_fleet_fault_hours_h3_kernel(
             nc.sync.dma_start(out=rows_bf[4 * which : 4 * which + 4, :], in_=vec.rearrange("(j c) -> j c", c=P))
 
         def load_exposure():
-            nc.sync.dma_start(out=expo[:], in_=exposure.rearrange("(g p t) -> p g t", p=P, t=PACK))
+            nc.sync.dma_start(out=expo_bf[0:4, :], in_=exposure.rearrange("(g m) -> g m", m=KP))
+
+        def expo_cast(engine):
+            copy_on(engine, expo_f32[:], expo_bf[:].rearrange("g (m t) -> g t m", t=PACK))
+
+        def expo_turn():
+            for t in range(PACK):
+                nc.tensor.transpose(expo[:, t, :], expo_f32[:, t, :], ident[:])
+
+        def expo_spill(engine):
+            copy_on(engine, expo_sb[:], expo[:, :, 0:4].rearrange("p t g -> p g t"))
 
         def rows_cast():
             nc.scalar.copy(out=rows_f32[:], in_=rows_bf[:])
@@ -306,271 +327,266 @@ def tile_fleet_fault_hours_h3_kernel(
 
         setup()
         load_readings(0,0,1)
-        load_readings(0,1,2)
-        load_signatures(0,0)
         T(0,0,0)
+        load_signatures(0,0)
         SI(0,0,"v",0,256)
-        C(0,0,"v")
-        load_signatures(0,1)
-        SI(0,0,"s",256,512)
-        SI(0,1,"s",0,256)
-        load_readings(0,2,3)
-        SI(0,1,"v",256,512)
+        load_readings(0,1,2)
         T(0,1,1)
+        load_signatures(0,1)
+        load_readings(0,2,3)
+        SI(0,0,"v",256,512)
+        C(0,0,"s")
         load_readings(0,3,4)
+        SI(0,1,"s",0,256)
+        load_efforts(0)
         load_signatures(1,0)
+        T(0,2,2)
+        load_exposure()
+        SI(0,1,"v",256,512)
         C(0,1,"s")
         SQ(0,0)
-        T(0,2,2)
         RQ(0,0,1)
-        T(0,3,3)
         SQ(0,1)
-        Z(0,0,0,4)
-        load_signatures(1,1)
-        RQ(0,1,2)
-        load_readings(1,0,2)
         C(0,2,"s")
-        SI(1,0,"s",0,256)
-        load_crew(1)
-        load_efforts(0)
-        Z(0,0,1,5)
-        RQ(0,2,3)
-        T(1,0,6)
-        T(1,1,7)
-        SI(1,0,"v",256,512)
-        SI(1,1,"s",0,256)
-        load_crew(0)
-        load_efforts(1)
-        C(0,3,"s")
-        SI(1,1,"v",256,512)
-        S(0,0,0)
-        SQ(1,0)
-        SQ(1,1)
-        rows_cast()
-        C(1,0,"s")
-        Z(0,0,2,0)
-        RQ(0,3,4)
-        S(0,0,1)
-        Z(0,1,0,1)
+        T(0,3,3)
         EI(0,0,"v",False)
-        S(0,0,2)
-        load_efforts(2)
-        C(1,1,"s")
         EI(0,1,"v",False)
-        EI(1,0,"v",False)
-        Z(0,1,1,2)
-        S(0,1,0)
+        RQ(0,1,2)
+        RQ(0,2,3)
+        Z(0,0,0,4)
+        C(0,3,"s")
         EQ(0,0,2)
-        EI(2,0,"v",False)
-        Z(0,0,3,3)
-        load_exposure()
+        Z(0,0,1,5)
+        RQ(0,3,4)
+        load_readings(1,0,2)
+        SI(1,0,"s",0,256)
+        Z(0,0,2,6)
+        load_signatures(1,1)
+        expo_cast("v")
+        SI(1,0,"v",256,512)
+        S(0,0,0)
+        SI(1,1,"v",0,256)
+        Z(0,0,3,0)
         load_readings(1,2,4)
-        load_readings(2,0,2)
-        load_readings(2,2,4)
-        Z(0,1,2,4)
-        S(0,1,1)
-        EI(1,1,"v",False)
-        S(0,1,2)
-        Z(0,1,3,6)
-        RQ(1,0,2)
-        rows_turn(5)
-        T(1,2,0)
-        rows_out()
-        EQ(1,0,2)
-        T(1,3,7)
-        T(2,0,1)
+        S(0,0,1)
+        T(1,0,1)
+        S(0,0,2)
         S(0,0,3)
-        M(0,0,0,256)
-        load_readings(3,0,2)
+        T(1,1,2)
+        SI(1,1,"v",256,512)
+        expo_turn()
+        T(1,2,3)
+        load_crew(0)
+        SQ(1,0)
+        load_readings(2,0,2)
+        C(1,0,"s")
+        load_readings(2,2,4)
+        SQ(1,1)
+        expo_spill("v")
+        T(1,3,4)
+        C(1,1,"s")
+        RQ(1,0,2)
         C(1,2,"s")
-        T(2,1,2)
-        T(2,2,4)
-        T(2,3,5)
-        Z(1,1,0,3)
-        Z(1,0,0,0)
-        S(0,1,3)
+        T(2,0,5)
+        T(2,1,6)
+        T(2,2,0)
+        T(2,3,1)
+        load_efforts(1)
+        Z(1,0,0,2)
         C(1,3,"s")
+        Z(1,0,1,3)
+        M(0,0)
         C(2,0,"s")
-        Z(1,1,1,6)
         C(2,2,"s")
-        rows_diff()
-        EI(2,1,"s",False)
-        M(0,1,0,256)
-        Z(1,0,1,7)
         RQ(1,2,4)
-        C(2,1,"s")
-        Z(1,0,2,1)
-        M(0,0,256,512)
-        C(2,3,"s")
-        load_readings(3,2,4)
-        S(1,0,0)
-        M(0,1,256,512)
-        S(1,0,1)
-        Z(1,1,2,4)
-        S(1,0,2)
-        Z(1,0,3,2)
-        Z(1,1,3,5)
-        S(1,0,3)
-        T(3,0,0)
+        C(2,1,"v")
+        load_crew(1)
+        Z(0,1,0,4)
+        Z(1,0,2,5)
+        EI(1,0,"v",False)
         RQ(2,0,2)
-        T(3,1,7)
-        T(3,2,1)
-        S(1,1,0)
-        HQ(0,0)
-        T(3,3,2)
-        C(3,0,"s")
-        S(1,1,1)
-        RQ(2,2,4)
-        EQ(2,0,2)
-        HQ(0,1)
-        S(1,1,2)
-        M(1,0,0,256)
-        D(0,1,0,1,3)
-        Z(2,0,0,0)
-        S(1,1,3)
-        C(3,1,"s")
-        load_skills(0)
-        S(2,0,0)
-        M(1,0,256,512)
-        M(1,1,0,256)
-        C(3,2,"s")
-        RQ(3,0,2)
-        Z(2,0,1,6)
-        Z(2,1,0,4)
-        S(2,0,1)
-        Z(2,0,2,5)
-        D(0,3,0,1,7)
-        S(2,0,2)
-        Z(2,0,3,0)
-        C(3,3,"s")
-        S(2,0,3)
-        Z(3,0,0,1)
-        Z(2,1,1,6)
-        D(0,2,0,1,5)
-        Z(3,0,1,2)
-        M(1,1,256,512)
-        S(2,1,0)
-        HQ(1,0)
-        D(0,3,1,2,None)
-        D(0,1,1,2,None)
-        RQ(3,2,4)
-        S(3,0,0)
-        M(2,0,0,256)
-        M(2,0,256,512)
-        S(2,1,1)
-        S(3,0,1)
-        HQ(1,1)
-        D(0,0,0,1,0)
-        HQ(2,0)
+        load_efforts(2)
+        Z(1,0,3,0)
+        C(2,3,"s")
+        S(1,0,0)
+        load_readings(3,0,2)
+        S(1,0,1)
+        S(0,1,0)
+        Z(0,1,1,1)
+        S(1,0,2)
+        Z(0,1,2,6)
+        S(1,0,3)
+        Z(2,0,0,2)
+        Z(2,0,1,3)
         load_efforts(3)
-        Z(3,0,2,4)
-        S(3,0,2)
-        Z(3,0,3,1)
-        S(3,0,3)
-        D(0,0,1,2,None)
-        M(3,0,0,256)
-        Z(2,1,2,6)
-        Z(2,1,3,2)
-        D(0,2,1,2,None)
-        EI(3,0,"s",False)
-        EI(3,1,"s",False)
-        S(2,1,2)
-        D(0,0,2,3,None)
-        S(2,1,3)
-        M(3,0,256,512)
-        EQ(3,0,2)
-        Z(3,1,0,4)
-        D(0,2,2,3,None)
-        D(0,3,2,3,None)
-        S(3,1,0)
-        Z(3,1,1,1)
-        HQ(3,0)
-        M(2,1,0,256)
-        Z(3,1,2,6)
-        S(3,1,1)
-        Z(3,1,3,2)
-        D(1,1,0,1,4)
-        D(0,0,3,4,None)
-        D(0,2,3,4,None)
-        S(3,1,2)
-        M(2,1,256,512)
-        S(3,1,3)
-        D(1,0,0,1,1)
-        M(3,1,0,256)
-        D(1,2,0,1,6)
-        D(0,3,3,4,None)
-        D(0,1,2,3,None)
-        D(0,1,3,4,None)
-        UM(0,0,2,"s2")
-        D(1,1,1,2,None)
-        HQ(2,1)
-        M(3,1,256,512)
-        D(1,2,1,2,None)
-        R(0,0,"s2")
-        D(1,0,1,2,None)
+        rows_cast()
+        S(0,1,1)
+        S(0,1,2)
+        Z(0,1,3,4)
+        load_readings(3,2,4)
+        T(3,0,5)
+        EI(2,0,"s",False)
+        EI(1,1,"v",False)
+        T(3,1,0)
+        S(0,1,3)
+        rows_turn(1)
+        C(3,0,"s")
+        T(3,2,6)
+        S(2,0,0)
+        S(2,0,1)
         load_skills(1)
+        C(3,1,"s")
+        HQ(0,0)
+        RQ(2,2,4)
+        T(3,3,4)
+        Z(2,0,2,5)
+        M(1,0)
+        S(2,0,2)
+        EI(2,1,"v",False)
+        HQ(1,0)
+        Z(2,0,3,2)
+        S(2,0,3)
+        Z(1,1,0,3)
+        C(3,2,"s")
+        EQ(1,0,2)
+        M(0,1)
+        C(3,3,"s")
+        Z(1,1,1,0)
+        Z(1,1,2,5)
+        RQ(3,0,2)
+        S(1,1,0)
+        Z(1,1,3,2)
+        Z(2,1,0,6)
+        S(1,1,1)
+        HQ(0,1)
+        EQ(2,0,2)
+        Z(3,0,0,4)
+        M(2,0)
+        Z(2,1,1,3)
+        S(1,1,2)
+        S(1,1,3)
+        D(0,0,0,1,0)
+        D(0,0,1,2,None)
+        RQ(3,2,4)
+        Z(3,0,1,5)
+        S(3,0,0)
+        S(2,1,0)
+        HQ(2,0)
+        S(3,0,1)
+        D(0,1,0,1,2)
+        S(2,1,1)
+        D(0,1,1,2,None)
+        Z(3,0,2,4)
+        EI(3,0,"v",False)
+        S(3,0,2)
+        M(1,1)
+        Z(3,0,3,6)
+        Z(2,1,2,5)
+        Z(2,1,3,3)
+        S(3,0,3)
+        rows_out()
+        HQ(1,1)
+        D(1,1,0,1,1)
+        rows_diff()
+        Z(3,1,0,4)
+        S(2,1,2)
+        M(3,0)
+        D(1,1,1,2,None)
+        D(0,2,0,1,6)
+        S(2,1,3)
+        Z(3,1,1,5)
+        D(0,2,1,2,None)
+        EI(3,1,"s",False)
+        load_skills(0)
+        D(0,1,2,3,None)
+        S(3,1,0)
+        Z(3,1,2,3)
+        HQ(3,0)
+        EQ(3,0,2)
+        Z(3,1,3,4)
+        M(2,1)
+        D(0,1,3,4,None)
+        S(3,1,1)
+        D(0,0,2,3,None)
+        S(3,1,2)
+        D(0,0,3,4,None)
+        D(0,2,2,3,None)
+        D(0,3,0,1,5)
+        R(0,0,"v")
+        S(3,1,3)
+        UM(0,0,3,"v")
+        R(0,1,"s2")
+        UM(0,1,4,"s2")
+        D(0,3,1,2,None)
+        D(0,2,3,4,None)
+        D(0,3,2,3,None)
+        D(0,3,3,4,None)
+        D(1,2,0,1,0)
         U(0,0)
-        UM(0,1,0,"s")
-        R(0,1,"s")
-        UM(0,2,3,"s")
-        Y(0,0)
-        store_y(0,0)
-        R(0,2,"s")
         U(0,1)
-        HQ(3,1)
-        U(0,2)
-        R(0,3,"s2")
-        Y(0,1)
-        D(1,0,2,3,None)
-        YB(0,0,"s")
-        D(1,3,0,1,5)
+        D(1,0,0,1,2)
+        HQ(2,1)
+        R(0,2,"s2")
         D(1,1,2,3,None)
-        UM(0,3,2,"s2")
-        U(0,3)
+        M(3,1)
+        D(1,2,1,2,None)
+        R(0,3,"s2")
+        UM(0,2,6,"s2")
+        Y(0,0)
+        D(1,0,1,2,None)
+        Y(0,1)
+        HQ(3,1)
+        D(1,0,2,3,None)
+        U(0,2)
+        YB(0,0,"s")
         Y(0,2)
+        UM(0,3,3,"s2")
+        store_y(0,0)
+        YB(0,1,"s")
+        U(0,3)
+        D(1,3,0,1,5)
+        D(1,3,1,2,None)
         D(1,0,3,4,None)
         store_y(0,1)
-        D(1,1,3,4,None)
-        D(1,3,1,2,None)
-        YB(0,1,"s")
-        D(1,3,2,3,None)
-        store_y(0,2)
-        Y(0,3)
         D(1,2,2,3,None)
-        YB(0,2,"s")
+        Y(0,3)
+        D(1,1,3,4,None)
+        store_y(0,2)
         R(1,0,"v")
-        UM(1,0,7,"v")
-        D(1,3,3,4,None)
+        UM(1,0,4,"v")
         D(1,2,3,4,None)
-        store_y(0,3)
-        R(1,1,"s")
+        R(1,1,"v")
+        D(1,3,2,3,None)
+        D(1,3,3,4,None)
+        UM(1,1,6,"v")
         U(1,0)
-        YB(0,3,"v")
+        YB(0,2,"s")
+        store_y(0,3)
+        YB(0,3,"s")
         R(1,2,"s")
-        UM(1,1,0,"s")
         YQ(0,0,4)
-        store_codes(0)
-        Y(1,0)
         U(1,1)
-        store_scales(0,0,nc.scalar)
-        store_scales(0,1,nc.sync)
         R(1,3,"s")
-        store_scales(0,2,nc.sync)
         UM(1,2,3,"s")
-        YB(1,0,"s")
         U(1,2)
-        store_scales(0,3,nc.sync)
-        Y(1,1)
         UM(1,3,2,"s")
+        store_scales(0,0,nc.scalar)
+        store_scales(0,1,nc.scalar)
+        Y(1,0)
+        Y(1,1)
         Y(1,2)
-        store_y(1,0)
-        YB(1,1,"s")
+        YB(1,0,"s")
         U(1,3)
-        YB(1,2,"s")
-        store_y(1,1)
-        store_y(1,2)
+        store_codes(0)
         Y(1,3)
+        store_y(1,0)
+        store_scales(0,2,nc.sync)
+        store_scales(0,3,nc.scalar)
+        YB(1,1,"s")
+        store_y(1,1)
         YQ(1,0,2)
+        store_y(1,2)
+        YB(1,2,"s")
         YB(1,3,"v")
         YQ(1,2,4)
         store_y(1,3)
@@ -578,4 +594,4 @@ def tile_fleet_fault_hours_h3_kernel(
         store_scales(1,1,nc.scalar)
         store_codes(1)
         store_scales(1,2,nc.sync)
-        store_scales(1,3,nc.scalar)
+        store_scales(1,3,nc.sync)

@@ -12,12 +12,19 @@ U32 = mybir.dt.uint32
 I32 = mybir.dt.int32
 U8 = mybir.dt.uint8
 FP8X4 = mybir.dt.float8_e4m3fn_x4
-ACT = mybir.ActivationFunctionType
+FUNC = mybir.ActivationFunctionType
 ALU = mybir.AluOpType
 
 P = 128
 PACK = 4
-KP = P * PACK
+GROUP = P * PACK
+HALF = GROUP // 2
+MACH_GROUPS = MACH // GROUP
+SENS_GROUPS = SENS // GROUP
+FAULT_GROUPS = FAULT // GROUP
+CREW_TILES = CREW // P
+ROTATING_BANKS = 7
+VECTOR_FAULTS = 400
 
 
 def tile_fleet_fault_hours_h3_kernel(
@@ -26,572 +33,436 @@ def tile_fleet_fault_hours_h3_kernel(
     nc = tc.nc
     with ExitStack() as ctx:
         keep = ctx.enter_context(tc.tile_pool(name="keep", bufs=1))
-        work = ctx.enter_context(tc.tile_pool(name="work", bufs=2))
+        work = ctx.enter_context(tc.tile_pool(name="work", bufs=1))
         psum = ctx.enter_context(tc.psum_pool(name="psum", bufs=1))
         ctx.enter_context(tc.manual_schedule())
 
         def kept(name, shape, dtype):
             return keep.tile(shape, dtype, name=name, align_bytes=64)
 
+        def kept_list(name, count, shape, dtype):
+            return [kept("%s%d" % (name, i), shape, dtype) for i in range(count)]
+
         ident = kept("ident", [P, P], F32)
-        warm = kept("warm", [P, 8], F32)
-        expo_bf = kept("expo_bf", [P, KP], BF16)
-        expo_f32 = kept("expo_f32", [P, PACK, P], F32)
-        expo_sb = kept("expo_sb", [P, 4, PACK], F32)
-        expo = psum.tile([P, PACK, P], F32, name="expo")
-        rows_bf = kept("rows_bf", [P, P], BF16)
-        rows_f32 = kept("rows_f32", [P, P], F32)
-        crew_cols = kept("crew_cols", [P, 8], F32)
-        plan_less_min = kept("plan_less_min", [P, 4], F32)
-        r_raw = [kept("r_raw%d" % g, [P, PACK, SENS], BF16) for g in range(4)]
-        r_codes = [kept("r_codes%d" % g, [P, PACK, 2, P], U32) for g in range(4)]
-        r_scales = [kept("r_scales%d" % g, [P, PACK, 2, P], U8) for g in range(4)]
-        s_raw = [[kept("s_raw%d%d" % (h, s), [P, PACK, KP], BF16) for s in range(2)] for h in range(2)]
-        s_codes = [kept("s_codes%d" % h, [P, 2, KP], U32) for h in range(2)]
-        s_scales = [kept("s_scales%d" % h, [P, 2, KP], U8) for h in range(2)]
-        e_raw = [kept("e_raw%d" % g, [P, PACK, CREW], BF16) for g in range(4)]
-        e_codes = [kept("e_codes%d" % j, [P, CREW], U32) for j in range(4)]
-        e_scales = [kept("e_scales%d" % j, [P, CREW], U8) for j in range(4)]
-        h_codes = [kept("h_codes%d" % h, [P, 4, KP], U32) for h in range(2)]
-        h_scales = [kept("h_scales%d" % h, [P, 4, KP], U8) for h in range(2)]
-        skill = [kept("skill%d" % h, [P, PACK, CREW], BF16) for h in range(2)]
-        y = [kept("y%d" % h, [P, 4, PACK, P], F32) for h in range(2)]
-        y_bf = [kept("y_bf%d" % h, [P, CREW, PACK], BF16) for h in range(2)]
-        y_codes = [kept("y_codes%d" % h, [P, CREW], U32) for h in range(2)]
-        y_scales = [kept("y_scales%d" % h, [P, CREW], U8) for h in range(2)]
+        warm = kept("warm", [P, 2], F32)
+        expo_rows = kept("expo_rows", [P, GROUP], BF16)
+        expo_rows_f32 = kept("expo_rows_f32", [P, PACK, P], F32)
+        expo_psum = psum.tile([P, PACK, P], F32, name="expo_psum")
+        expo_sbuf = kept("expo_sbuf", [P, MACH_GROUPS, PACK], F32)
+        crew_rows = kept("crew_rows", [P, P], BF16)
+        crew_rows_f32 = kept("crew_rows_f32", [P, P], F32)
+        crew_cols = kept("crew_cols", [P, 2 * CREW_TILES], F32)
+        plan_less_min = kept("plan_less_min", [P, CREW_TILES], F32)
+        read_raw = kept_list("read_raw", MACH_GROUPS, [P, PACK, SENS], BF16)
+        read_codes = kept_list("read_codes", MACH_GROUPS, [P, PACK, SENS_GROUPS, P], U32)
+        read_scales = kept_list("read_scales", MACH_GROUPS, [P, PACK, SENS_GROUPS, P], U8)
+        sign_raw = [kept_list("sign_raw%d" % f, SENS_GROUPS, [P, PACK, GROUP], BF16) for f in range(FAULT_GROUPS)]
+        sign_codes = kept_list("sign_codes", FAULT_GROUPS, [P, SENS_GROUPS, GROUP], U32)
+        sign_scales = kept_list("sign_scales", FAULT_GROUPS, [P, SENS_GROUPS, GROUP], U8)
+        eff_raw = kept_list("eff_raw", MACH_GROUPS, [P, PACK, CREW], BF16)
+        eff_codes = kept_list("eff_codes", MACH_GROUPS, [P, CREW], U32)
+        eff_scales = kept_list("eff_scales", MACH_GROUPS, [P, CREW], U8)
+        h_codes = kept_list("h_codes", FAULT_GROUPS, [P, MACH_GROUPS, GROUP], U32)
+        h_scales = kept_list("h_scales", FAULT_GROUPS, [P, MACH_GROUPS, GROUP], U8)
+        skill = kept_list("skill", FAULT_GROUPS, [P, PACK, CREW], BF16)
+        y = kept_list("y", FAULT_GROUPS, [P, CREW_TILES, PACK, P], F32)
+        y_grouped = kept_list("y_grouped", FAULT_GROUPS, [P, CREW, PACK], BF16)
+        y_codes = kept_list("y_codes", FAULT_GROUPS, [P, CREW], U32)
+        y_scales = kept_list("y_scales", FAULT_GROUPS, [P, CREW], U8)
+
         live = {}
+        free_banks = list(range(ROTATING_BANKS))
 
-        def bank(b):
-            return psum.tile([P, KP], F32, name="bank%d" % b)
+        def take_bank(key):
+            number = free_banks[0]
+            free_banks.remove(number)
+            live[key] = (psum.tile([P, GROUP], F32, name="bank%d" % number), number)
+            return live[key][0]
 
-        def grouped():
-            return work.tile([P, KP * PACK], BF16, name="grouped", bufs=5, align_bytes=64)
+        def empty_bank(key):
+            free_banks.append(live[key][1])
+            return live[key][0]
 
-        def copy_on(engine, out, in_):
-            if engine == "v":
-                nc.vector.tensor_copy(out=out, in_=in_)
-            else:
-                nc.scalar.copy(out=out, in_=in_)
+        def grouped_tile(key, opens):
+            if opens:
+                live[key] = work.tile([P, GROUP * PACK], BF16, name="grouped", bufs=5, align_bytes=64)
+            return live[key]
+
+        def on_vector(out, in_):
+            nc.vector.tensor_copy(out=out, in_=in_)
+
+        def on_scalar(out, in_):
+            nc.scalar.copy(out=out, in_=in_)
 
         def quantize(codes, scales, in_):
             nc.vector.quantize_mx(out=codes.bitcast(FP8X4), scales=scales, in_=in_)
 
-        def load_readings(g, t0, t1):
-            rows = readings[KP * g : KP * (g + 1), :].rearrange("(p t) k -> p t k", t=PACK)
-            nc.sync.dma_start(out=r_raw[g][:, t0:t1, :], in_=rows[:, t0:t1, :])
+        def group_rows(copy, dst, src):
+            copy(dst.rearrange("p (c i t) -> p c t i", i=4, t=PACK), src.rearrange("p t (c i) -> p c t i", i=4))
 
-        def load_signatures(h, s):
-            rows = signatures[KP * s : KP * (s + 1), KP * h : KP * (h + 1)]
-            nc.sync.dma_start(out=s_raw[h][s][:], in_=rows.rearrange("(p t) f -> p t f", t=PACK))
+        def rows_of_group(tensor, index):
+            return tensor[GROUP * index : GROUP * (index + 1), :].rearrange("(p t) c -> p t c", t=PACK)
+
+        def load_readings(g, t0, t1):
+            nc.sync.dma_start(out=read_raw[g][:, t0:t1, :], in_=rows_of_group(readings, g)[:, t0:t1, :])
+
+        def load_signatures(f, s):
+            nc.sync.dma_start(out=sign_raw[f][s][:], in_=rows_of_group(signatures, s)[:, :, GROUP * f : GROUP * (f + 1)])
 
         def load_efforts(g):
-            rows = efforts[KP * g : KP * (g + 1), :]
-            nc.sync.dma_start(out=e_raw[g][:], in_=rows.rearrange("(p t) c -> p t c", t=PACK))
+            nc.sync.dma_start(out=eff_raw[g][:], in_=rows_of_group(efforts, g))
 
-        def load_skills(h):
-            rows = skills[KP * h : KP * (h + 1), :]
-            nc.sync.dma_start(out=skill[h][:], in_=rows.rearrange("(p t) c -> p t c", t=PACK))
-
-        def T(g, t, b):
-            words = r_raw[g][:, t, :].bitcast(F32)
-            turned = bank(b)
-            live["T", g, t] = turned
-            for s in range(2):
-                for u in range(2):
-                    q = 2 * s + u
-                    nc.tensor.transpose(
-                        turned[:, P * q : P * (q + 1)], words[:, 256 * s + u : 256 * (s + 1) : 2], ident[:]
-                    )
-
-        def C(g, t, engine="s"):
-            if t % 2 == 0:
-                live["rg", g, t // 2] = grouped()
-            dst = live["rg", g, t // 2][:, 1024 * (t % 2) : 1024 * (t % 2 + 1)].bitcast(F32)
-            copy_on(
-                engine,
-                dst.rearrange("p (s r u) -> p s r u", s=2, u=2),
-                live["T", g, t][:].rearrange("p (s u r) -> p s r u", s=2, u=2),
-            )
-
-        def RQ(g, t0, t1):
-            src = live["rg", g, t0 // 2][:, 1024 * (t0 % 2) : 1024 * (t0 % 2 + t1 - t0)]
-            quantize(
-                r_codes[g][:, t0:t1, :, :].rearrange("p t s r -> p (t s r)"),
-                r_scales[g][:, t0:t1, :, :].rearrange("p t s r -> p (t s r)"),
-                src,
-            )
-
-        def SI(h, s, engine, c0=0, c1=KP):
-            if c0 == 0:
-                live["sg", h, s] = grouped()
-            dst = live["sg", h, s][:, PACK * c0 : PACK * c1]
-            copy_on(
-                engine,
-                dst.rearrange("p (c i t) -> p c t i", i=4, t=PACK),
-                s_raw[h][s][:, :, c0:c1].rearrange("p t (c i) -> p c t i", i=4),
-            )
-
-        def SQ(h, s):
-            quantize(s_codes[h][:, s, :], s_scales[h][:, s, :], live["sg", h, s][:])
-
-        def EI(g, a, engine, chained):
-            if a == 0:
-                live["eg", g] = grouped()
-            copy_on(
-                engine,
-                live["eg", g][:, 1024 * a : 1024 * (a + 1)].rearrange("p (c i t) -> p c t i", i=4, t=PACK),
-                e_raw[g][:, :, 256 * a : 256 * (a + 1)].rearrange("p t (c i) -> p c t i", i=4),
-            )
-
-        def EQ(g, a0, a1):
-            quantize(e_codes[g][:], e_scales[g][:], live["eg", g][:])
-
-        def Z(g, h, t, b):
-            z = bank(b)
-            live["z", g, h, t] = z
-            for s in range(2):
-                nc.tensor.matmul_mx(
-                    out=z[:],
-                    lhsT=r_codes[g][:, t, s, :].bitcast(FP8X4),
-                    lhsT_scale=r_scales[g][:, t, s, :],
-                    rhs=s_codes[h][:, s, :].bitcast(FP8X4),
-                    rhs_scale=s_scales[h][:, s, :],
-                    start=(s == 0),
-                    stop=(s == 1),
-                )
-
-        def S(g, h, t):
-            if t == 0:
-                live["sig", g, h] = work.tile([P, PACK, KP], F32, name="sig", bufs=3)
-            nc.scalar.activation(out=live["sig", g, h][:, t, :], in_=live["z", g, h, t][:], func=ACT.Sigmoid)
-
-        def M(g, h):
-            h_bf = work.tile([P, KP * PACK], BF16, name="h_bf", bufs=1, align_bytes=64)
-            live["hg", g, h] = h_bf
-            sig = live["sig", g, h]
-            split = 384
-            nc.gpsimd.tensor_tensor(
-                out=h_bf[:, PACK * split :].rearrange("p (c t) -> p c t", t=PACK),
-                in0=sig[:, :, split:].rearrange("p t c -> p c t"),
-                in1=expo_sb[:, g : g + 1, :].broadcast_to([P, KP - split, PACK]),
-                op=ALU.mult,
-            )
-            nc.vector.tensor_tensor(
-                out=h_bf[:, : PACK * split].rearrange("p (c i t) -> p c t i", i=2, t=PACK),
-                in0=sig[:, :, :split].rearrange("p t (c i) -> p c t i", i=2),
-                in1=expo[:, :, g : g + 1].unsqueeze(1).broadcast_to([P, split // 2, PACK, 2]),
-                op=ALU.mult,
-            )
-
-        def HQ(g, h, c0=0, c1=KP):
-            quantize(h_codes[h][:, g, c0:c1], h_scales[h][:, g, c0:c1], live["hg", g, h][:, PACK * c0 : PACK * c1])
-
-        def D(h, j, g0, g1, b=None):
-            if g0 == 0:
-                live["d", h, j] = bank(b)
-            for g in range(g0, g1):
-                nc.tensor.matmul_mx(
-                    out=live["d", h, j][:],
-                    lhsT=e_codes[g][:, P * j : P * (j + 1)].bitcast(FP8X4),
-                    lhsT_scale=e_scales[g][:, P * j : P * (j + 1)],
-                    rhs=h_codes[h][:, g, :].bitcast(FP8X4),
-                    rhs_scale=h_scales[h][:, g, :],
-                    start=(g == 0),
-                    stop=(g == 3),
-                )
-
-        def R(h, j, engine):
-            above = work.tile([P, PACK, P], F32, name="above", bufs=3)
-            live["r", h, j] = above
-            if engine == "v":
-                nc.vector.tensor_scalar(
-                    out=above[:],
-                    in0=live["d", h, j][:].rearrange("p (m t) -> p t m", t=PACK),
-                    scalar1=crew_cols[:, j : j + 1],
-                    scalar2=crew_cols[:, 4 + j : 5 + j],
-                    op0=ALU.add,
-                    op1=ALU.max,
-                )
-                return
-            nc.scalar.activation(
-                out=above[:],
-                in_=live["d", h, j][:].rearrange("p (m t) -> p t m", t=PACK),
-                func=ACT.Relu,
-                bias=plan_less_min[:, j : j + 1],
-            )
-            if engine == "s2":
-                nc.scalar.activation(
-                    out=above[:], in_=above[:], func=ACT.Identity, bias=crew_cols[:, 4 + j : 5 + j]
-                )
-
-        def UM(h, j, b, engine):
-            hours = bank(b)
-            live["u", h, j] = hours
-            live["fresh", h, j] = engine != "s"
-            if engine != "s":
-                return
-            for t in range(PACK):
-                nc.tensor.matmul(
-                    hours[:, P * t : P * (t + 1)],
-                    lhsT=crew_cols[:, 4 + j : 5 + j].to_broadcast([P, P]),
-                    rhs=ident[:],
-                    start=(t == 0),
-                    stop=False,
-                    is_transpose=True,
-                )
-
-        def U(h, j):
-            for t in range(PACK):
-                nc.tensor.matmul(
-                    live["u", h, j][:, P * t : P * (t + 1)],
-                    lhsT=live["r", h, j][:, t, :],
-                    rhs=ident[:],
-                    start=live["fresh", h, j],
-                    stop=(live["fresh", h, j] or t == PACK - 1),
-                    is_transpose=True,
-                )
-
-        def Y(h, j):
-            cols = slice(P * j, P * (j + 1))
-            nc.vector.tensor_tensor(
-                out=y[h][:, j, :, :],
-                in0=live["u", h, j][:].rearrange("p (t c) -> p t c", t=PACK),
-                in1=skill[h][:, :, cols],
-                op=ALU.mult,
-            )
-
-        def YB(h, j, engine):
-            copy_on(
-                engine,
-                y_bf[h][:, P * j : P * (j + 1), :].rearrange("p (c i) t -> p c t i", i=4),
-                y[h][:, j, :, :].rearrange("p t (c i) -> p c t i", i=4),
-            )
-
-        def YQ(h, j0, j1):
-            cols = slice(P * j0, P * j1)
-            quantize(y_codes[h][:, cols], y_scales[h][:, cols], y_bf[h][:, cols, :].rearrange("p c t -> p (c t)"))
-
-        def store_y(h, j):
-            cols = slice(P * j, P * (j + 1))
-            rows = out_0[KP * h : KP * (h + 1), :].rearrange("(p t) c -> p t c", t=PACK)
-            nc.sync.dma_start(out=rows[:, :, cols], in_=y[h][:, j, :, :])
-
-        def store_codes(h):
-            words = out_1[h].rearrange("p m t -> p (m t)").bitcast(I32)
-            nc.sync.dma_start(out=words, in_=y_codes[h][:].bitcast(I32))
-
-        def store_scales(h, quad, queue):
-            queue.dma_start(
-                out=out_2[h, 4 * quad : 4 * quad + 4, :].bitcast(I32),
-                in_=y_scales[h][32 * quad : 32 * quad + 4, :].bitcast(I32),
-            )
-
-        def setup():
-            nc.vector.memset(warm[:], 0.0)
-            nc.gpsimd.memset(rows_bf[:], 0.0)
-            make_identity(nc, ident[:])
-            nc.gpsimd.memset(expo_bf[:], 0.0)
-            nc.scalar.activation(out=warm[:, 4:5], in_=warm[:, 0:1], func=ACT.Sigmoid)
-
-        def load_crew(which):
-            vec = (plan, minimum)[which]
-            nc.sync.dma_start(out=rows_bf[4 * which : 4 * which + 4, :], in_=vec.rearrange("(j c) -> j c", c=P))
+        def load_skills(f):
+            nc.sync.dma_start(out=skill[f][:], in_=rows_of_group(skills, f))
 
         def load_exposure():
-            nc.sync.dma_start(out=expo_bf[0:4, :], in_=exposure.rearrange("(g m) -> g m", m=KP))
+            nc.sync.dma_start(out=expo_rows[0:MACH_GROUPS, :], in_=exposure.rearrange("(g m) -> g m", m=GROUP))
 
-        def expo_cast(engine):
-            copy_on(engine, expo_f32[:], expo_bf[:].rearrange("g (m t) -> g t m", t=PACK))
+        def load_crew_rows():
+            for i, vector in enumerate((plan, minimum)):
+                rows = crew_rows[CREW_TILES * i : CREW_TILES * (i + 1), :]
+                nc.sync.dma_start(out=rows, in_=vector.rearrange("(j c) -> j c", c=P))
 
-        def expo_turn():
+        def cast_exposure():
+            on_scalar(expo_rows_f32[:], expo_rows[:].rearrange("g (m t) -> g t m", t=PACK))
+
+        def turn_exposure():
             for t in range(PACK):
-                nc.tensor.transpose(expo[:, t, :], expo_f32[:, t, :], ident[:])
+                nc.tensor.transpose(expo_psum[:, t, :], expo_rows_f32[:, t, :], ident[:])
 
-        def expo_spill(engine):
-            copy_on(engine, expo_sb[:], expo[:, :, 0:4].rearrange("p t g -> p g t"))
+        def spill_exposure():
+            on_vector(expo_sbuf[:], expo_psum[:, :, 0:MACH_GROUPS].rearrange("p t g -> p g t"))
 
-        def rows_cast():
-            nc.scalar.copy(out=rows_f32[:], in_=rows_bf[:])
+        def cast_crew_rows():
+            on_scalar(crew_rows_f32[:], crew_rows[:])
 
-        def rows_turn(b):
-            live["rows"] = bank(b)
-            nc.tensor.transpose(live["rows"][:, 0:P], rows_f32[:], ident[:])
+        def turn_crew_rows():
+            nc.tensor.transpose(take_bank("crew")[:, 0:P], crew_rows_f32[:], ident[:])
 
-        def rows_out():
-            nc.vector.tensor_copy(out=crew_cols[:], in_=live["rows"][:, 0:8])
+        def spill_crew_cols():
+            on_vector(crew_cols[:], empty_bank("crew")[:, 0 : 2 * CREW_TILES])
 
-        def rows_diff():
+        def subtract_minimum():
             nc.vector.tensor_tensor(
-                out=plan_less_min[:], in0=crew_cols[:, 0:4], in1=crew_cols[:, 4:8], op=ALU.subtract
+                out=plan_less_min[:], in0=crew_cols[:, :CREW_TILES], in1=crew_cols[:, CREW_TILES:], op=ALU.subtract
             )
 
-        setup()
-        load_readings(0,0,1)
-        T(0,0,0)
-        load_signatures(0,0)
-        SI(0,0,"v",0,256)
-        load_readings(0,1,2)
-        T(0,1,1)
-        load_signatures(0,1)
-        load_readings(0,2,3)
-        SI(0,0,"v",256,512)
-        C(0,0,"s")
-        load_readings(0,3,4)
-        SI(0,1,"s",0,256)
-        load_efforts(0)
-        load_signatures(1,0)
-        T(0,2,2)
+        def turn_readings(g, ts):
+            for t in ts:
+                words = read_raw[g][:, t, :].bitcast(F32)
+                bank = take_bank(("turned", g, t))
+                for s in range(SENS_GROUPS):
+                    for u in range(2):
+                        slot = 2 * s + u
+                        every_second = words[:, 2 * P * s + u : 2 * P * (s + 1) : 2]
+                        nc.tensor.transpose(bank[:, P * slot : P * (slot + 1)], every_second, ident[:])
+            for t in ts:
+                pair = grouped_tile(("readings", g, t // 2), t % 2 == 0)
+                dst = pair[:, SENS * (t % 2) : SENS * (t % 2 + 1)].bitcast(F32)
+                on_scalar(
+                    dst.rearrange("p (s m u) -> p s m u", s=SENS_GROUPS, u=2),
+                    empty_bank(("turned", g, t))[:].rearrange("p (s u m) -> p s m u", s=SENS_GROUPS, u=2),
+                )
+
+        def quantize_readings(g, t0, t1):
+            first = t0 % 2
+            quantize(
+                read_codes[g][:, t0:t1, :, :].rearrange("p t s m -> p (t s m)"),
+                read_scales[g][:, t0:t1, :, :].rearrange("p t s m -> p (t s m)"),
+                live["readings", g, t0 // 2][:, SENS * first : SENS * (first + t1 - t0)],
+            )
+
+        def group_signatures(f, s, half, copy):
+            tile = grouped_tile(("signatures", f, s), half == 0)
+            c0, c1 = HALF * half, HALF * (half + 1)
+            group_rows(copy, tile[:, PACK * c0 : PACK * c1], sign_raw[f][s][:, :, c0:c1])
+
+        def quantize_signatures(f, s):
+            quantize(sign_codes[f][:, s, :], sign_scales[f][:, s, :], live["signatures", f, s][:])
+
+        def group_efforts(g, half, copy):
+            tile = grouped_tile(("efforts", g), half == 0)
+            c0, c1 = HALF * half, HALF * (half + 1)
+            group_rows(copy, tile[:, PACK * c0 : PACK * c1], eff_raw[g][:, :, c0:c1])
+
+        def quantize_efforts(g):
+            quantize(eff_codes[g][:], eff_scales[g][:], live["efforts", g][:])
+
+        def score(g, f, ts=range(PACK)):
+            for t in ts:
+                z = take_bank(("z", g, f, t))
+                for s in range(SENS_GROUPS):
+                    nc.tensor.matmul_mx(
+                        out=z[:],
+                        lhsT=read_codes[g][:, t, s, :].bitcast(FP8X4),
+                        lhsT_scale=read_scales[g][:, t, s, :],
+                        rhs=sign_codes[f][:, s, :].bitcast(FP8X4),
+                        rhs_scale=sign_scales[f][:, s, :],
+                        start=(s == 0),
+                        stop=(s == SENS_GROUPS - 1),
+                    )
+                if t == 0:
+                    live["sigmoid", g, f] = work.tile([P, PACK, GROUP], F32, name="sigmoid", bufs=4)
+                nc.scalar.activation(
+                    out=live["sigmoid", g, f][:, t, :], in_=empty_bank(("z", g, f, t))[:], func=FUNC.Sigmoid
+                )
+
+        def weigh(g, f):
+            h_grouped = work.tile([P, GROUP * PACK], BF16, name="h_grouped", bufs=1, align_bytes=64)
+            live["h", g, f] = h_grouped
+            sigmoid = live["sigmoid", g, f]
+            nc.gpsimd.tensor_tensor(
+                out=h_grouped[:, PACK * VECTOR_FAULTS :].rearrange("p (c t) -> p c t", t=PACK),
+                in0=sigmoid[:, :, VECTOR_FAULTS:].rearrange("p t c -> p c t"),
+                in1=expo_sbuf[:, g : g + 1, :].broadcast_to([P, GROUP - VECTOR_FAULTS, PACK]),
+                op=ALU.mult,
+            )
+            nc.vector.tensor_tensor(
+                out=h_grouped[:, : PACK * VECTOR_FAULTS].rearrange("p (c i t) -> p c t i", i=2, t=PACK),
+                in0=sigmoid[:, :, :VECTOR_FAULTS].rearrange("p t (c i) -> p c t i", i=2),
+                in1=expo_psum[:, :, g : g + 1].unsqueeze(1).broadcast_to([P, VECTOR_FAULTS // 2, PACK, 2]),
+                op=ALU.mult,
+            )
+
+        def quantize_h(g, f):
+            quantize(h_codes[f][:, g, :], h_scales[f][:, g, :], live["h", g, f][:])
+
+        def add_up(f, js, gs):
+            for j in js:
+                for g in gs:
+                    d = take_bank(("d", f, j)) if g == 0 else live["d", f, j][0]
+                    nc.tensor.matmul_mx(
+                        out=d[:],
+                        lhsT=eff_codes[g][:, P * j : P * (j + 1)].bitcast(FP8X4),
+                        lhsT_scale=eff_scales[g][:, P * j : P * (j + 1)],
+                        rhs=h_codes[f][:, g, :].bitcast(FP8X4),
+                        rhs_scale=h_scales[f][:, g, :],
+                        start=(g == 0),
+                        stop=(g == MACH_GROUPS - 1),
+                    )
+
+        def hours_operands(f, j):
+            live["hours", f, j] = work.tile([P, PACK, P], F32, name="hours", bufs=3)
+            return live["hours", f, j][:], empty_bank(("d", f, j))[:].rearrange("p (m t) -> p t m", t=PACK)
+
+        def floor_on_vector(f, j):
+            hours, d = hours_operands(f, j)
+            nc.vector.tensor_scalar(
+                out=hours,
+                in0=d,
+                scalar1=crew_cols[:, j : j + 1],
+                scalar2=crew_cols[:, CREW_TILES + j : CREW_TILES + j + 1],
+                op0=ALU.add,
+                op1=ALU.max,
+            )
+
+        def floor_on_scalar(f, j):
+            hours, d = hours_operands(f, j)
+            nc.scalar.activation(out=hours, in_=d, func=FUNC.Relu, bias=plan_less_min[:, j : j + 1])
+            nc.scalar.activation(
+                out=hours, in_=hours, func=FUNC.Identity, bias=crew_cols[:, CREW_TILES + j : CREW_TILES + j + 1]
+            )
+
+        def turn_hours(f, j):
+            bank = take_bank(("hours_turned", f, j))
+            for t in range(PACK):
+                nc.tensor.transpose(bank[:, P * t : P * (t + 1)], live["hours", f, j][:, t, :], ident[:])
+
+        def finish_y(f, j):
+            crews = slice(P * j, P * (j + 1))
+            nc.vector.tensor_tensor(
+                out=y[f][:, j, :, :],
+                in0=empty_bank(("hours_turned", f, j))[:].rearrange("p (t c) -> p t c", t=PACK),
+                in1=skill[f][:, :, crews],
+                op=ALU.mult,
+            )
+            nc.sync.dma_start(out=rows_of_group(out_0, f)[:, :, crews], in_=y[f][:, j, :, :])
+
+        def group_y(f, j, copy):
+            dst = y_grouped[f][:, P * j : P * (j + 1), :].rearrange("p c t -> p (c t)")
+            group_rows(copy, dst, y[f][:, j, :, :])
+
+        def quantize_y(f, j0, j1):
+            crews = slice(P * j0, P * j1)
+            quantize(y_codes[f][:, crews], y_scales[f][:, crews], y_grouped[f][:, crews, :].rearrange("p c t -> p (c t)"))
+
+        def store_codes(f, j0, j1):
+            crews = slice(P * j0, P * j1)
+            words = out_1[f].rearrange("p m t -> p (m t)").bitcast(I32)
+            nc.sync.dma_start(out=words[:, crews], in_=y_codes[f][:, crews].bitcast(I32))
+
+        def store_scales(f, queues):
+            for quad, queue in enumerate(queues):
+                queue.dma_start(
+                    out=out_2[f, 4 * quad : 4 * quad + 4, :].bitcast(I32),
+                    in_=y_scales[f][32 * quad : 32 * quad + 4, :].bitcast(I32),
+                )
+
+        nc.vector.memset(warm[:], 0.0)
+        nc.gpsimd.memset(crew_rows[:], 0.0)
+        make_identity(nc, ident[:])
+        nc.gpsimd.memset(expo_rows[:], 0.0)
+        nc.scalar.activation(out=warm[:, 1:2], in_=warm[:, 0:1], func=FUNC.Sigmoid)
+
+        load_readings(0, 0, 1)
+        load_signatures(0, 0)
+        load_signatures(0, 1)
+        for t in range(1, PACK):
+            load_readings(0, t, t + 1)
+        load_signatures(1, 0)
+        load_signatures(1, 1)
         load_exposure()
-        SI(0,1,"v",256,512)
-        C(0,1,"s")
-        SQ(0,0)
-        RQ(0,0,1)
-        SQ(0,1)
-        C(0,2,"s")
-        T(0,3,3)
-        EI(0,0,"v",False)
-        EI(0,1,"v",False)
-        RQ(0,1,2)
-        RQ(0,2,3)
-        Z(0,0,0,4)
-        C(0,3,"s")
-        EQ(0,0,2)
-        Z(0,0,1,5)
-        RQ(0,3,4)
-        load_readings(1,0,2)
-        SI(1,0,"s",0,256)
-        Z(0,0,2,6)
-        load_signatures(1,1)
-        expo_cast("v")
-        SI(1,0,"v",256,512)
-        S(0,0,0)
-        SI(1,1,"v",0,256)
-        Z(0,0,3,0)
-        load_readings(1,2,4)
-        S(0,0,1)
-        T(1,0,1)
-        S(0,0,2)
-        S(0,0,3)
-        T(1,1,2)
-        SI(1,1,"v",256,512)
-        expo_turn()
-        T(1,2,3)
-        load_crew(0)
-        SQ(1,0)
-        load_readings(2,0,2)
-        C(1,0,"s")
-        load_readings(2,2,4)
-        SQ(1,1)
-        expo_spill("v")
-        T(1,3,4)
-        C(1,1,"s")
-        RQ(1,0,2)
-        C(1,2,"s")
-        T(2,0,5)
-        T(2,1,6)
-        T(2,2,0)
-        T(2,3,1)
+        load_readings(1, 0, 2)
+        load_efforts(0)
         load_efforts(1)
-        Z(1,0,0,2)
-        C(1,3,"s")
-        Z(1,0,1,3)
-        M(0,0)
-        C(2,0,"s")
-        C(2,2,"s")
-        RQ(1,2,4)
-        C(2,1,"v")
-        load_crew(1)
-        Z(0,1,0,4)
-        Z(1,0,2,5)
-        EI(1,0,"v",False)
-        RQ(2,0,2)
+        load_readings(1, 2, 4)
+        load_readings(2, 0, 2)
+        load_readings(2, 2, 4)
+        load_crew_rows()
+        load_readings(3, 0, 2)
         load_efforts(2)
-        Z(1,0,3,0)
-        C(2,3,"s")
-        S(1,0,0)
-        load_readings(3,0,2)
-        S(1,0,1)
-        S(0,1,0)
-        Z(0,1,1,1)
-        S(1,0,2)
-        Z(0,1,2,6)
-        S(1,0,3)
-        Z(2,0,0,2)
-        Z(2,0,1,3)
+        load_readings(3, 2, 4)
         load_efforts(3)
-        rows_cast()
-        S(0,1,1)
-        S(0,1,2)
-        Z(0,1,3,4)
-        load_readings(3,2,4)
-        T(3,0,5)
-        EI(2,0,"s",False)
-        EI(1,1,"v",False)
-        T(3,1,0)
-        S(0,1,3)
-        rows_turn(1)
-        C(3,0,"s")
-        T(3,2,6)
-        S(2,0,0)
-        S(2,0,1)
-        load_skills(1)
-        C(3,1,"s")
-        HQ(0,0)
-        RQ(2,2,4)
-        T(3,3,4)
-        Z(2,0,2,5)
-        M(1,0)
-        S(2,0,2)
-        EI(2,1,"v",False)
-        HQ(1,0)
-        Z(2,0,3,2)
-        S(2,0,3)
-        Z(1,1,0,3)
-        C(3,2,"s")
-        EQ(1,0,2)
-        M(0,1)
-        C(3,3,"s")
-        Z(1,1,1,0)
-        Z(1,1,2,5)
-        RQ(3,0,2)
-        S(1,1,0)
-        Z(1,1,3,2)
-        Z(2,1,0,6)
-        S(1,1,1)
-        HQ(0,1)
-        EQ(2,0,2)
-        Z(3,0,0,4)
-        M(2,0)
-        Z(2,1,1,3)
-        S(1,1,2)
-        S(1,1,3)
-        D(0,0,0,1,0)
-        D(0,0,1,2,None)
-        RQ(3,2,4)
-        Z(3,0,1,5)
-        S(3,0,0)
-        S(2,1,0)
-        HQ(2,0)
-        S(3,0,1)
-        D(0,1,0,1,2)
-        S(2,1,1)
-        D(0,1,1,2,None)
-        Z(3,0,2,4)
-        EI(3,0,"v",False)
-        S(3,0,2)
-        M(1,1)
-        Z(3,0,3,6)
-        Z(2,1,2,5)
-        Z(2,1,3,3)
-        S(3,0,3)
-        rows_out()
-        HQ(1,1)
-        D(1,1,0,1,1)
-        rows_diff()
-        Z(3,1,0,4)
-        S(2,1,2)
-        M(3,0)
-        D(1,1,1,2,None)
-        D(0,2,0,1,6)
-        S(2,1,3)
-        Z(3,1,1,5)
-        D(0,2,1,2,None)
-        EI(3,1,"s",False)
         load_skills(0)
-        D(0,1,2,3,None)
-        S(3,1,0)
-        Z(3,1,2,3)
-        HQ(3,0)
-        EQ(3,0,2)
-        Z(3,1,3,4)
-        M(2,1)
-        D(0,1,3,4,None)
-        S(3,1,1)
-        D(0,0,2,3,None)
-        S(3,1,2)
-        D(0,0,3,4,None)
-        D(0,2,2,3,None)
-        D(0,3,0,1,5)
-        R(0,0,"v")
-        S(3,1,3)
-        UM(0,0,3,"v")
-        R(0,1,"s2")
-        UM(0,1,4,"s2")
-        D(0,3,1,2,None)
-        D(0,2,3,4,None)
-        D(0,3,2,3,None)
-        D(0,3,3,4,None)
-        D(1,2,0,1,0)
-        U(0,0)
-        U(0,1)
-        D(1,0,0,1,2)
-        HQ(2,1)
-        R(0,2,"s2")
-        D(1,1,2,3,None)
-        M(3,1)
-        D(1,2,1,2,None)
-        R(0,3,"s2")
-        UM(0,2,6,"s2")
-        Y(0,0)
-        D(1,0,1,2,None)
-        Y(0,1)
-        HQ(3,1)
-        D(1,0,2,3,None)
-        U(0,2)
-        YB(0,0,"s")
-        Y(0,2)
-        UM(0,3,3,"s2")
-        store_y(0,0)
-        YB(0,1,"s")
-        U(0,3)
-        D(1,3,0,1,5)
-        D(1,3,1,2,None)
-        D(1,0,3,4,None)
-        store_y(0,1)
-        D(1,2,2,3,None)
-        Y(0,3)
-        D(1,1,3,4,None)
-        store_y(0,2)
-        R(1,0,"v")
-        UM(1,0,4,"v")
-        D(1,2,3,4,None)
-        R(1,1,"v")
-        D(1,3,2,3,None)
-        D(1,3,3,4,None)
-        UM(1,1,6,"v")
-        U(1,0)
-        YB(0,2,"s")
-        store_y(0,3)
-        YB(0,3,"s")
-        R(1,2,"s")
-        YQ(0,0,4)
-        U(1,1)
-        R(1,3,"s")
-        UM(1,2,3,"s")
-        U(1,2)
-        UM(1,3,2,"s")
-        store_scales(0,0,nc.scalar)
-        store_scales(0,1,nc.scalar)
-        Y(1,0)
-        Y(1,1)
-        Y(1,2)
-        YB(1,0,"s")
-        U(1,3)
-        store_codes(0)
-        Y(1,3)
-        store_y(1,0)
-        store_scales(0,2,nc.sync)
-        store_scales(0,3,nc.scalar)
-        YB(1,1,"s")
-        store_y(1,1)
-        YQ(1,0,2)
-        store_y(1,2)
-        YB(1,2,"s")
-        YB(1,3,"v")
-        YQ(1,2,4)
-        store_y(1,3)
-        store_scales(1,0,nc.scalar)
-        store_scales(1,1,nc.scalar)
-        store_codes(1)
-        store_scales(1,2,nc.sync)
-        store_scales(1,3,nc.sync)
+        load_skills(1)
+
+        turn_readings(0, [0])
+        group_signatures(0, 0, 0, on_vector)
+        quantize_readings(0, 0, 1)
+        group_signatures(0, 0, 1, on_vector)
+        group_signatures(0, 1, 0, on_scalar)
+        group_signatures(0, 1, 1, on_vector)
+        quantize_signatures(0, 0)
+        quantize_signatures(0, 1)
+        for t in range(1, PACK):
+            turn_readings(0, [t])
+        quantize_readings(0, 1, 2)
+        group_signatures(1, 0, 0, on_vector)
+        group_signatures(1, 0, 1, on_scalar)
+        quantize_readings(0, 2, 3)
+        group_signatures(1, 1, 0, on_vector)
+        quantize_readings(0, 3, 4)
+        group_signatures(1, 1, 1, on_vector)
+        quantize_signatures(1, 0)
+        quantize_signatures(1, 1)
+        score(0, 0, [0, 1])
+        cast_exposure()
+        score(0, 0, [2, 3])
+        turn_readings(1, [0, 1])
+        turn_exposure()
+        score(0, 1, [0, 1])
+        turn_readings(1, [2, 3])
+        group_efforts(0, 0, on_vector)
+        group_efforts(0, 1, on_vector)
+        group_efforts(1, 0, on_vector)
+        spill_exposure()
+        quantize_readings(1, 0, 2)
+
+        weigh(0, 0)
+        quantize_readings(1, 2, 4)
+        turn_readings(2, [0, 1])
+        score(1, 0)
+        group_efforts(1, 1, on_vector)
+        quantize_readings(2, 0, 2)
+        quantize_efforts(0)
+        quantize_h(0, 0)
+        quantize_efforts(1)
+
+        weigh(1, 0)
+        turn_readings(2, [2, 3])
+        turn_readings(3, [0, 1])
+        score(0, 1, [2, 3])
+        group_efforts(2, 0, on_vector)
+        quantize_h(1, 0)
+        quantize_readings(2, 2, 4)
+
+        weigh(0, 1)
+        score(2, 0, [0, 1])
+        score(1, 1, [0, 1])
+        score(2, 0, [2, 3])
+        quantize_h(0, 1)
+        quantize_readings(3, 0, 2)
+
+        weigh(2, 0)
+        cast_crew_rows()
+        score(1, 1, [2, 3])
+        turn_readings(3, [2, 3])
+        turn_crew_rows()
+        spill_crew_cols()
+        quantize_h(2, 0)
+        quantize_readings(3, 2, 4)
+
+        weigh(1, 1)
+        score(3, 0, [0, 1])
+        score(2, 1, [0, 1])
+        score(3, 0, [2, 3])
+        group_efforts(2, 1, on_vector)
+        quantize_h(1, 1)
+        quantize_efforts(2)
+
+        weigh(3, 0)
+        add_up(0, [3, 0, 2], [0, 1])
+        group_efforts(3, 0, on_scalar)
+        group_efforts(3, 1, on_scalar)
+        score(2, 1, [2, 3])
+        subtract_minimum()
+        quantize_h(3, 0)
+        quantize_efforts(3)
+
+        weigh(2, 1)
+        score(3, 1, [0, 1])
+        add_up(0, [2], [2])
+        add_up(0, [1], [0, 1])
+        score(3, 1, [2, 3])
+        add_up(0, [1, 0], [2, 3])
+        add_up(0, [2], [3])
+        add_up(0, [3], [2, 3])
+        quantize_h(2, 1)
+        floor_on_vector(0, 0)
+
+        weigh(3, 1)
+        floor_on_scalar(0, 1)
+        floor_on_scalar(0, 2)
+        add_up(1, [2], [0, 1, 2])
+        turn_hours(0, 0)
+        turn_hours(0, 1)
+        floor_on_scalar(0, 3)
+        add_up(1, [1, 0], [0, 1, 2])
+        quantize_h(3, 1)
+
+        finish_y(0, 0)
+        finish_y(0, 1)
+        add_up(1, [0], [3])
+        turn_hours(0, 2)
+        turn_hours(0, 3)
+        add_up(1, [2, 1], [3])
+        add_up(1, [3], [0, 1, 2])
+        group_y(0, 0, on_vector)
+        finish_y(0, 2)
+        finish_y(0, 3)
+        floor_on_scalar(1, 0)
+        for j in range(1, CREW_TILES):
+            group_y(0, j, on_scalar)
+        turn_hours(1, 0)
+        floor_on_vector(1, 1)
+        floor_on_vector(1, 2)
+        add_up(1, [3], [3])
+        floor_on_scalar(1, 3)
+        for j in range(1, CREW_TILES):
+            turn_hours(1, j)
+        finish_y(1, 0)
+        quantize_y(0, 0, 4)
+        store_codes(0, 0, 4)
+        store_scales(0, [nc.sync] * 4)
+        group_y(1, 0, on_scalar)
+        finish_y(1, 1)
+        finish_y(1, 2)
+        group_y(1, 1, on_vector)
+        group_y(1, 2, on_scalar)
+        finish_y(1, 3)
+        quantize_y(1, 0, 2)
+        store_codes(1, 0, 2)
+        group_y(1, 3, on_vector)
+        quantize_y(1, 2, 4)
+        store_codes(1, 2, 4)
+        store_scales(1, [nc.scalar, nc.sync] * 2)

@@ -24,7 +24,7 @@ SENS_GROUPS = SENS // GROUP
 FAULT_GROUPS = FAULT // GROUP
 CREW_TILES = CREW // P
 ROTATING_BANKS = 7
-VECTOR_FAULTS = 400
+VECTOR_FAULTS = 384
 
 
 def tile_fleet_fault_hours_h3_kernel(
@@ -107,7 +107,8 @@ def tile_fleet_fault_hours_h3_kernel(
             nc.sync.dma_start(out=read_raw[g][:, t0:t1, :], in_=rows_of_group(readings, g)[:, t0:t1, :])
 
         def load_signatures(f, s):
-            nc.sync.dma_start(out=sign_raw[f][s][:], in_=rows_of_group(signatures, s)[:, :, GROUP * f : GROUP * (f + 1)])
+            faults = slice(GROUP * f, GROUP * (f + 1))
+            nc.sync.dma_start(out=sign_raw[f][s][:], in_=rows_of_group(signatures, s)[:, :, faults])
 
         def load_efforts(g):
             nc.sync.dma_start(out=eff_raw[g][:], in_=rows_of_group(efforts, g))
@@ -118,10 +119,9 @@ def tile_fleet_fault_hours_h3_kernel(
         def load_exposure():
             nc.sync.dma_start(out=expo_rows[0:MACH_GROUPS, :], in_=exposure.rearrange("(g m) -> g m", m=GROUP))
 
-        def load_crew_rows():
-            for i, vector in enumerate((plan, minimum)):
-                rows = crew_rows[CREW_TILES * i : CREW_TILES * (i + 1), :]
-                nc.sync.dma_start(out=rows, in_=vector.rearrange("(j c) -> j c", c=P))
+        def load_crew_rows(vector, first_row):
+            rows = crew_rows[first_row : first_row + CREW_TILES, :]
+            nc.sync.dma_start(out=rows, in_=vector.rearrange("(j c) -> j c", c=P))
 
         def cast_exposure():
             on_scalar(expo_rows_f32[:], expo_rows[:].rearrange("g (m t) -> g t m", t=PACK))
@@ -147,7 +147,7 @@ def tile_fleet_fault_hours_h3_kernel(
                 out=plan_less_min[:], in0=crew_cols[:, :CREW_TILES], in1=crew_cols[:, CREW_TILES:], op=ALU.subtract
             )
 
-        def turn_readings(g, ts):
+        def turn_readings(g, ts, copy=on_scalar):
             for t in ts:
                 words = read_raw[g][:, t, :].bitcast(F32)
                 bank = take_bank(("turned", g, t))
@@ -159,7 +159,7 @@ def tile_fleet_fault_hours_h3_kernel(
             for t in ts:
                 pair = grouped_tile(("readings", g, t // 2), t % 2 == 0)
                 dst = pair[:, SENS * (t % 2) : SENS * (t % 2 + 1)].bitcast(F32)
-                on_scalar(
+                copy(
                     dst.rearrange("p (s m u) -> p s m u", s=SENS_GROUPS, u=2),
                     empty_bank(("turned", g, t))[:].rearrange("p (s u m) -> p s m u", s=SENS_GROUPS, u=2),
                 )
@@ -227,19 +227,18 @@ def tile_fleet_fault_hours_h3_kernel(
         def quantize_h(g, f):
             quantize(h_codes[f][:, g, :], h_scales[f][:, g, :], live["h", g, f][:])
 
-        def add_up(f, js, gs):
-            for j in js:
-                for g in gs:
-                    d = take_bank(("d", f, j)) if g == 0 else live["d", f, j][0]
-                    nc.tensor.matmul_mx(
-                        out=d[:],
-                        lhsT=eff_codes[g][:, P * j : P * (j + 1)].bitcast(FP8X4),
-                        lhsT_scale=eff_scales[g][:, P * j : P * (j + 1)],
-                        rhs=h_codes[f][:, g, :].bitcast(FP8X4),
-                        rhs_scale=h_scales[f][:, g, :],
-                        start=(g == 0),
-                        stop=(g == MACH_GROUPS - 1),
-                    )
+        def add_up(f, j, gs):
+            for g in gs:
+                d = take_bank(("d", f, j)) if g == 0 else live["d", f, j][0]
+                nc.tensor.matmul_mx(
+                    out=d[:],
+                    lhsT=eff_codes[g][:, P * j : P * (j + 1)].bitcast(FP8X4),
+                    lhsT_scale=eff_scales[g][:, P * j : P * (j + 1)],
+                    rhs=h_codes[f][:, g, :].bitcast(FP8X4),
+                    rhs_scale=h_scales[f][:, g, :],
+                    start=(g == 0),
+                    stop=(g == MACH_GROUPS - 1),
+                )
 
         def hours_operands(f, j):
             live["hours", f, j] = work.tile([P, PACK, P], F32, name="hours", bufs=3)
@@ -256,9 +255,13 @@ def tile_fleet_fault_hours_h3_kernel(
                 op1=ALU.max,
             )
 
-        def floor_on_scalar(f, j):
+        def excess_on_scalar(f, j):
             hours, d = hours_operands(f, j)
             nc.scalar.activation(out=hours, in_=d, func=FUNC.Relu, bias=plan_less_min[:, j : j + 1])
+
+        def floor_on_scalar(f, j):
+            excess_on_scalar(f, j)
+            hours = live["hours", f, j][:]
             nc.scalar.activation(
                 out=hours, in_=hours, func=FUNC.Identity, bias=crew_cols[:, CREW_TILES + j : CREW_TILES + j + 1]
             )
@@ -267,6 +270,31 @@ def tile_fleet_fault_hours_h3_kernel(
             bank = take_bank(("hours_turned", f, j))
             for t in range(PACK):
                 nc.tensor.transpose(bank[:, P * t : P * (t + 1)], live["hours", f, j][:, t, :], ident[:])
+
+        def lay_minimum(f, j):
+            bank = take_bank(("hours_turned", f, j))
+            column = crew_cols[:, CREW_TILES + j : CREW_TILES + j + 1].to_broadcast([P, P])
+            for t in range(PACK):
+                nc.tensor.matmul(
+                    bank[:, P * t : P * (t + 1)],
+                    lhsT=column,
+                    rhs=ident[:],
+                    start=(t == 0),
+                    stop=False,
+                    is_transpose=True,
+                )
+
+        def turn_excess(f, j):
+            bank = live["hours_turned", f, j][0]
+            for t in range(PACK):
+                nc.tensor.matmul(
+                    bank[:, P * t : P * (t + 1)],
+                    lhsT=live["hours", f, j][:, t, :],
+                    rhs=ident[:],
+                    start=False,
+                    stop=(t == PACK - 1),
+                    is_transpose=True,
+                )
 
         def finish_y(f, j):
             crews = slice(P * j, P * (j + 1))
@@ -284,7 +312,8 @@ def tile_fleet_fault_hours_h3_kernel(
 
         def quantize_y(f, j0, j1):
             crews = slice(P * j0, P * j1)
-            quantize(y_codes[f][:, crews], y_scales[f][:, crews], y_grouped[f][:, crews, :].rearrange("p c t -> p (c t)"))
+            grouped = y_grouped[f][:, crews, :].rearrange("p c t -> p (c t)")
+            quantize(y_codes[f][:, crews], y_scales[f][:, crews], grouped)
 
         def store_codes(f, j0, j1):
             crews = slice(P * j0, P * j1)
@@ -305,164 +334,179 @@ def tile_fleet_fault_hours_h3_kernel(
         nc.scalar.activation(out=warm[:, 1:2], in_=warm[:, 0:1], func=FUNC.Sigmoid)
 
         load_readings(0, 0, 1)
+        load_readings(0, 1, 2)
+        load_readings(0, 2, 3)
         load_signatures(0, 0)
         load_signatures(0, 1)
-        for t in range(1, PACK):
-            load_readings(0, t, t + 1)
-        load_signatures(1, 0)
-        load_signatures(1, 1)
-        load_exposure()
+        load_readings(0, 3, 4)
         load_readings(1, 0, 2)
+        load_signatures(1, 0)
+        load_exposure()
+        load_signatures(1, 1)
+        load_readings(1, 2, 4)
         load_efforts(0)
         load_efforts(1)
-        load_readings(1, 2, 4)
+        load_crew_rows(plan, 0)
+        load_crew_rows(minimum, CREW_TILES)
         load_readings(2, 0, 2)
-        load_readings(2, 2, 4)
-        load_crew_rows()
-        load_readings(3, 0, 2)
         load_efforts(2)
+        load_readings(2, 2, 4)
+        load_readings(3, 0, 2)
         load_readings(3, 2, 4)
         load_efforts(3)
         load_skills(0)
         load_skills(1)
 
-        turn_readings(0, [0])
-        group_signatures(0, 0, 0, on_vector)
+        turn_readings(0, [0], on_vector)
         quantize_readings(0, 0, 1)
-        group_signatures(0, 0, 1, on_vector)
-        group_signatures(0, 1, 0, on_scalar)
-        group_signatures(0, 1, 1, on_vector)
-        quantize_signatures(0, 0)
-        quantize_signatures(0, 1)
-        for t in range(1, PACK):
-            turn_readings(0, [t])
+        turn_readings(0, [1])
         quantize_readings(0, 1, 2)
-        group_signatures(1, 0, 0, on_vector)
-        group_signatures(1, 0, 1, on_scalar)
+        group_signatures(0, 0, 0, on_scalar)
+        turn_readings(0, [2])
+        group_signatures(0, 1, 0, on_scalar)
+        group_signatures(0, 0, 1, on_vector)
+        group_signatures(0, 1, 1, on_vector)
+        turn_readings(0, [3])
+        turn_readings(1, [0, 1])
+        cast_exposure()
+        quantize_signatures(0, 0)
         quantize_readings(0, 2, 3)
-        group_signatures(1, 1, 0, on_vector)
+        quantize_signatures(0, 1)
         quantize_readings(0, 3, 4)
+        group_signatures(1, 0, 0, on_vector)
+        group_signatures(1, 0, 1, on_vector)
+        quantize_readings(1, 0, 2)
+        group_signatures(1, 1, 0, on_scalar)
         group_signatures(1, 1, 1, on_vector)
         quantize_signatures(1, 0)
-        quantize_signatures(1, 1)
         score(0, 0, [0, 1])
-        cast_exposure()
-        score(0, 0, [2, 3])
-        turn_readings(1, [0, 1])
-        turn_exposure()
-        score(0, 1, [0, 1])
-        turn_readings(1, [2, 3])
+        quantize_signatures(1, 1)
         group_efforts(0, 0, on_vector)
+        turn_exposure()
+        turn_readings(1, [2, 3])
+        score(0, 0, [2, 3])
         group_efforts(0, 1, on_vector)
-        group_efforts(1, 0, on_vector)
+        quantize_readings(1, 2, 4)
+        score(1, 0, [0, 1])
         spill_exposure()
-        quantize_readings(1, 0, 2)
+        group_efforts(1, 0, on_vector)
 
         weigh(0, 0)
-        quantize_readings(1, 2, 4)
-        turn_readings(2, [0, 1])
-        score(1, 0)
+        score(0, 1, [0, 1])
         group_efforts(1, 1, on_vector)
-        quantize_readings(2, 0, 2)
-        quantize_efforts(0)
+        score(1, 0, [2, 3])
+        cast_crew_rows()
         quantize_h(0, 0)
-        quantize_efforts(1)
+        score(0, 1, [2, 3])
+        quantize_efforts(0)
 
         weigh(1, 0)
-        turn_readings(2, [2, 3])
-        turn_readings(3, [0, 1])
-        score(0, 1, [2, 3])
-        group_efforts(2, 0, on_vector)
+        turn_readings(2, [0, 1])
+        turn_crew_rows()
+        quantize_efforts(1)
         quantize_h(1, 0)
-        quantize_readings(2, 2, 4)
+        quantize_readings(2, 0, 2)
 
         weigh(0, 1)
-        score(2, 0, [0, 1])
-        score(1, 1, [0, 1])
-        score(2, 0, [2, 3])
+        turn_readings(2, [2, 3])
+        score(1, 1)
+        group_efforts(2, 0, on_vector)
+        turn_readings(3, [0, 1])
         quantize_h(0, 1)
-        quantize_readings(3, 0, 2)
-
-        weigh(2, 0)
-        cast_crew_rows()
-        score(1, 1, [2, 3])
-        turn_readings(3, [2, 3])
-        turn_crew_rows()
-        spill_crew_cols()
-        quantize_h(2, 0)
-        quantize_readings(3, 2, 4)
+        quantize_readings(2, 2, 4)
 
         weigh(1, 1)
-        score(3, 0, [0, 1])
+        quantize_readings(3, 0, 2)
+        turn_readings(3, [2, 3])
+        score(2, 0, [0, 1])
+        quantize_h(1, 1)
+        quantize_readings(3, 2, 4)
+        score(2, 0, [2, 3])
         score(2, 1, [0, 1])
+        score(3, 0, [0, 1])
+
+        weigh(2, 0)
         score(3, 0, [2, 3])
         group_efforts(2, 1, on_vector)
-        quantize_h(1, 1)
+        add_up(0, 1, [0, 1])
+        quantize_h(2, 0)
         quantize_efforts(2)
+        add_up(0, 0, [0, 1])
+        add_up(0, 2, [0, 1])
+        group_efforts(3, 0, on_scalar)
+        spill_crew_cols()
+        group_efforts(3, 1, on_scalar)
 
         weigh(3, 0)
-        add_up(0, [3, 0, 2], [0, 1])
-        group_efforts(3, 0, on_scalar)
-        group_efforts(3, 1, on_scalar)
         score(2, 1, [2, 3])
+        add_up(0, 1, [2])
         subtract_minimum()
         quantize_h(3, 0)
         quantize_efforts(3)
+        add_up(0, 2, [2])
+        add_up(0, 0, [2])
 
         weigh(2, 1)
         score(3, 1, [0, 1])
-        add_up(0, [2], [2])
-        add_up(0, [1], [0, 1])
-        score(3, 1, [2, 3])
-        add_up(0, [1, 0], [2, 3])
-        add_up(0, [2], [3])
-        add_up(0, [3], [2, 3])
         quantize_h(2, 1)
-        floor_on_vector(0, 0)
+        score(3, 1, [2, 3])
+        add_up(0, 0, [3])
+        add_up(0, 3, [0, 1, 2])
+        add_up(0, 1, [3])
+        add_up(0, 3, [3])
+        add_up(0, 2, [3])
+        floor_on_scalar(0, 0)
+        floor_on_vector(0, 1)
+        add_up(1, 2, [0, 1, 2])
+        turn_hours(0, 0)
 
         weigh(3, 1)
-        floor_on_scalar(0, 1)
+        finish_y(0, 0)
         floor_on_scalar(0, 2)
-        add_up(1, [2], [0, 1, 2])
-        turn_hours(0, 0)
-        turn_hours(0, 1)
         floor_on_scalar(0, 3)
-        add_up(1, [1, 0], [0, 1, 2])
+        turn_hours(0, 1)
         quantize_h(3, 1)
 
-        finish_y(0, 0)
         finish_y(0, 1)
-        add_up(1, [0], [3])
+        group_y(0, 0, on_scalar)
+        add_up(1, 0, [0, 1, 2])
+        add_up(1, 1, [0, 1, 2])
         turn_hours(0, 2)
-        turn_hours(0, 3)
-        add_up(1, [2, 1], [3])
-        add_up(1, [3], [0, 1, 2])
-        group_y(0, 0, on_vector)
         finish_y(0, 2)
+        group_y(0, 1, on_scalar)
+        turn_hours(0, 3)
+        group_y(0, 2, on_scalar)
         finish_y(0, 3)
-        floor_on_scalar(1, 0)
-        for j in range(1, CREW_TILES):
-            group_y(0, j, on_scalar)
-        turn_hours(1, 0)
-        floor_on_vector(1, 1)
-        floor_on_vector(1, 2)
-        add_up(1, [3], [3])
-        floor_on_scalar(1, 3)
-        for j in range(1, CREW_TILES):
-            turn_hours(1, j)
-        finish_y(1, 0)
+        add_up(1, 0, [3])
+        group_y(0, 3, on_scalar)
+        add_up(1, 1, [3])
+        floor_on_vector(1, 0)
         quantize_y(0, 0, 4)
+        add_up(1, 3, [0, 1, 2])
+        add_up(1, 2, [3])
+        add_up(1, 3, [3])
+        excess_on_scalar(1, 1)
+        turn_hours(1, 0)
+        lay_minimum(1, 1)
+        turn_excess(1, 1)
+        excess_on_scalar(1, 2)
+        lay_minimum(1, 2)
         store_codes(0, 0, 4)
+        excess_on_scalar(1, 3)
+        turn_excess(1, 2)
         store_scales(0, [nc.sync] * 4)
+        finish_y(1, 0)
         group_y(1, 0, on_scalar)
+        lay_minimum(1, 3)
         finish_y(1, 1)
+        turn_excess(1, 3)
         finish_y(1, 2)
-        group_y(1, 1, on_vector)
-        group_y(1, 2, on_scalar)
         finish_y(1, 3)
+        group_y(1, 1, on_scalar)
         quantize_y(1, 0, 2)
-        store_codes(1, 0, 2)
+        group_y(1, 2, on_scalar)
         group_y(1, 3, on_vector)
         quantize_y(1, 2, 4)
+        store_codes(1, 0, 2)
         store_codes(1, 2, 4)
-        store_scales(1, [nc.scalar, nc.sync] * 2)
+        store_scales(1, [nc.sync, nc.sync, nc.scalar, nc.scalar])

from contextlib import ExitStack

import concourse.mybir as mybir
from concourse.masks import make_identity

MACH, SENS, FAULT, CREW = 2048, 1024, 1024, 512
FLOPS = 2 * MACH * SENS * FAULT + 2 * FAULT * MACH * CREW

F32 = mybir.dt.float32
BF16 = mybir.dt.bfloat16
U32 = mybir.dt.uint32
I32 = mybir.dt.int32
U8 = mybir.dt.uint8
FP8X4 = mybir.dt.float8_e4m3fn_x4
FUNC = mybir.ActivationFunctionType
ALU = mybir.AluOpType

P = 128
PACK = 4
GROUP = P * PACK
HALF = GROUP // 2
MACH_GROUPS = MACH // GROUP
SENS_GROUPS = SENS // GROUP
FAULT_GROUPS = FAULT // GROUP
CREW_TILES = CREW // P
ROTATING_BANKS = 7
VECTOR_FAULTS = 384


def tile_fleet_fault_hours_h3_kernel(
    tc, readings, signatures, exposure, efforts, plan, minimum, skills, out_0, out_1, out_2
):
    nc = tc.nc
    with ExitStack() as ctx:
        keep = ctx.enter_context(tc.tile_pool(name="keep", bufs=1))
        work = ctx.enter_context(tc.tile_pool(name="work", bufs=1))
        psum = ctx.enter_context(tc.psum_pool(name="psum", bufs=1))
        ctx.enter_context(tc.manual_schedule())

        def kept(name, shape, dtype):
            return keep.tile(shape, dtype, name=name, align_bytes=64)

        def kept_list(name, count, shape, dtype):
            return [kept("%s%d" % (name, i), shape, dtype) for i in range(count)]

        ident = kept("ident", [P, P], F32)
        warm = kept("warm", [P, 2], F32)
        expo_rows = kept("expo_rows", [P, GROUP], BF16)
        expo_rows_f32 = kept("expo_rows_f32", [P, PACK, P], F32)
        expo_psum = psum.tile([P, PACK, P], F32, name="expo_psum")
        expo_sbuf = kept("expo_sbuf", [P, MACH_GROUPS, PACK], F32)
        crew_rows = kept("crew_rows", [P, P], BF16)
        crew_rows_f32 = kept("crew_rows_f32", [P, P], F32)
        crew_cols = kept("crew_cols", [P, 2 * CREW_TILES], F32)
        plan_less_min = kept("plan_less_min", [P, CREW_TILES], F32)
        read_raw = kept_list("read_raw", MACH_GROUPS, [P, PACK, SENS], BF16)
        read_codes = kept_list("read_codes", MACH_GROUPS, [P, PACK, SENS_GROUPS, P], U32)
        read_scales = kept_list("read_scales", MACH_GROUPS, [P, PACK, SENS_GROUPS, P], U8)
        sign_raw = [kept_list("sign_raw%d" % f, SENS_GROUPS, [P, PACK, GROUP], BF16) for f in range(FAULT_GROUPS)]
        sign_codes = kept_list("sign_codes", FAULT_GROUPS, [P, SENS_GROUPS, GROUP], U32)
        sign_scales = kept_list("sign_scales", FAULT_GROUPS, [P, SENS_GROUPS, GROUP], U8)
        eff_raw = kept_list("eff_raw", MACH_GROUPS, [P, PACK, CREW], BF16)
        eff_codes = kept_list("eff_codes", MACH_GROUPS, [P, CREW], U32)
        eff_scales = kept_list("eff_scales", MACH_GROUPS, [P, CREW], U8)
        h_codes = kept_list("h_codes", FAULT_GROUPS, [P, MACH_GROUPS, GROUP], U32)
        h_scales = kept_list("h_scales", FAULT_GROUPS, [P, MACH_GROUPS, GROUP], U8)
        skill = kept_list("skill", FAULT_GROUPS, [P, PACK, CREW], BF16)
        y = kept_list("y", FAULT_GROUPS, [P, CREW_TILES, PACK, P], F32)
        y_grouped = kept_list("y_grouped", FAULT_GROUPS, [P, CREW, PACK], BF16)
        y_codes = kept_list("y_codes", FAULT_GROUPS, [P, CREW], U32)
        y_scales = kept_list("y_scales", FAULT_GROUPS, [P, CREW], U8)

        live = {}
        free_banks = list(range(ROTATING_BANKS))

        def take_bank(key):
            number = free_banks[0]
            free_banks.remove(number)
            live[key] = (psum.tile([P, GROUP], F32, name="bank%d" % number), number)
            return live[key][0]

        def empty_bank(key):
            free_banks.append(live[key][1])
            return live[key][0]

        def grouped_tile(key, opens):
            if opens:
                live[key] = work.tile([P, GROUP * PACK], BF16, name="grouped", bufs=5, align_bytes=64)
            return live[key]

        def on_vector(out, in_):
            nc.vector.tensor_copy(out=out, in_=in_)

        def on_scalar(out, in_):
            nc.scalar.copy(out=out, in_=in_)

        def quantize(codes, scales, in_):
            nc.vector.quantize_mx(out=codes.bitcast(FP8X4), scales=scales, in_=in_)

        def group_rows(copy, dst, src):
            copy(dst.rearrange("p (c i t) -> p c t i", i=4, t=PACK), src.rearrange("p t (c i) -> p c t i", i=4))

        def rows_of_group(tensor, index):
            return tensor[GROUP * index : GROUP * (index + 1), :].rearrange("(p t) c -> p t c", t=PACK)

        def load_readings(g, t0, t1):
            nc.sync.dma_start(out=read_raw[g][:, t0:t1, :], in_=rows_of_group(readings, g)[:, t0:t1, :])

        def load_signatures(f, s):
            faults = slice(GROUP * f, GROUP * (f + 1))
            nc.sync.dma_start(out=sign_raw[f][s][:], in_=rows_of_group(signatures, s)[:, :, faults])

        def load_efforts(g):
            nc.sync.dma_start(out=eff_raw[g][:], in_=rows_of_group(efforts, g))

        def load_skills(f):
            nc.sync.dma_start(out=skill[f][:], in_=rows_of_group(skills, f))

        def load_exposure():
            nc.sync.dma_start(out=expo_rows[0:MACH_GROUPS, :], in_=exposure.rearrange("(g m) -> g m", m=GROUP))

        def load_crew_rows(vector, first_row):
            rows = crew_rows[first_row : first_row + CREW_TILES, :]
            nc.sync.dma_start(out=rows, in_=vector.rearrange("(j c) -> j c", c=P))

        def cast_exposure():
            on_scalar(expo_rows_f32[:], expo_rows[:].rearrange("g (m t) -> g t m", t=PACK))

        def turn_exposure():
            for t in range(PACK):
                nc.tensor.transpose(expo_psum[:, t, :], expo_rows_f32[:, t, :], ident[:])

        def spill_exposure():
            on_vector(expo_sbuf[:], expo_psum[:, :, 0:MACH_GROUPS].rearrange("p t g -> p g t"))

        def cast_crew_rows():
            on_scalar(crew_rows_f32[:], crew_rows[:])

        def turn_crew_rows():
            nc.tensor.transpose(take_bank("crew")[:, 0:P], crew_rows_f32[:], ident[:])

        def spill_crew_cols():
            on_vector(crew_cols[:], empty_bank("crew")[:, 0 : 2 * CREW_TILES])

        def subtract_minimum():
            nc.vector.tensor_tensor(
                out=plan_less_min[:], in0=crew_cols[:, :CREW_TILES], in1=crew_cols[:, CREW_TILES:], op=ALU.subtract
            )

        def turn_readings(g, ts, copy=on_scalar):
            for t in ts:
                words = read_raw[g][:, t, :].bitcast(F32)
                bank = take_bank(("turned", g, t))
                for s in range(SENS_GROUPS):
                    for u in range(2):
                        slot = 2 * s + u
                        every_second = words[:, 2 * P * s + u : 2 * P * (s + 1) : 2]
                        nc.tensor.transpose(bank[:, P * slot : P * (slot + 1)], every_second, ident[:])
            for t in ts:
                pair = grouped_tile(("readings", g, t // 2), t % 2 == 0)
                dst = pair[:, SENS * (t % 2) : SENS * (t % 2 + 1)].bitcast(F32)
                copy(
                    dst.rearrange("p (s m u) -> p s m u", s=SENS_GROUPS, u=2),
                    empty_bank(("turned", g, t))[:].rearrange("p (s u m) -> p s m u", s=SENS_GROUPS, u=2),
                )

        def quantize_readings(g, t0, t1):
            first = t0 % 2
            quantize(
                read_codes[g][:, t0:t1, :, :].rearrange("p t s m -> p (t s m)"),
                read_scales[g][:, t0:t1, :, :].rearrange("p t s m -> p (t s m)"),
                live["readings", g, t0 // 2][:, SENS * first : SENS * (first + t1 - t0)],
            )

        def group_signatures(f, s, half, copy):
            tile = grouped_tile(("signatures", f, s), half == 0)
            c0, c1 = HALF * half, HALF * (half + 1)
            group_rows(copy, tile[:, PACK * c0 : PACK * c1], sign_raw[f][s][:, :, c0:c1])

        def quantize_signatures(f, s):
            quantize(sign_codes[f][:, s, :], sign_scales[f][:, s, :], live["signatures", f, s][:])

        def group_efforts(g, half, copy):
            tile = grouped_tile(("efforts", g), half == 0)
            c0, c1 = HALF * half, HALF * (half + 1)
            group_rows(copy, tile[:, PACK * c0 : PACK * c1], eff_raw[g][:, :, c0:c1])

        def quantize_efforts(g):
            quantize(eff_codes[g][:], eff_scales[g][:], live["efforts", g][:])

        def score(g, f, ts=range(PACK)):
            for t in ts:
                z = take_bank(("z", g, f, t))
                for s in range(SENS_GROUPS):
                    nc.tensor.matmul_mx(
                        out=z[:],
                        lhsT=read_codes[g][:, t, s, :].bitcast(FP8X4),
                        lhsT_scale=read_scales[g][:, t, s, :],
                        rhs=sign_codes[f][:, s, :].bitcast(FP8X4),
                        rhs_scale=sign_scales[f][:, s, :],
                        start=(s == 0),
                        stop=(s == SENS_GROUPS - 1),
                    )
                if t == 0:
                    live["sigmoid", g, f] = work.tile([P, PACK, GROUP], F32, name="sigmoid", bufs=4)
                nc.scalar.activation(
                    out=live["sigmoid", g, f][:, t, :], in_=empty_bank(("z", g, f, t))[:], func=FUNC.Sigmoid
                )

        def weigh(g, f):
            h_grouped = work.tile([P, GROUP * PACK], BF16, name="h_grouped", bufs=1, align_bytes=64)
            live["h", g, f] = h_grouped
            sigmoid = live["sigmoid", g, f]
            nc.gpsimd.tensor_tensor(
                out=h_grouped[:, PACK * VECTOR_FAULTS :].rearrange("p (c t) -> p c t", t=PACK),
                in0=sigmoid[:, :, VECTOR_FAULTS:].rearrange("p t c -> p c t"),
                in1=expo_sbuf[:, g : g + 1, :].broadcast_to([P, GROUP - VECTOR_FAULTS, PACK]),
                op=ALU.mult,
            )
            nc.vector.tensor_tensor(
                out=h_grouped[:, : PACK * VECTOR_FAULTS].rearrange("p (c i t) -> p c t i", i=2, t=PACK),
                in0=sigmoid[:, :, :VECTOR_FAULTS].rearrange("p t (c i) -> p c t i", i=2),
                in1=expo_psum[:, :, g : g + 1].unsqueeze(1).broadcast_to([P, VECTOR_FAULTS // 2, PACK, 2]),
                op=ALU.mult,
            )

        def quantize_h(g, f):
            quantize(h_codes[f][:, g, :], h_scales[f][:, g, :], live["h", g, f][:])

        def add_up(f, j, gs):
            for g in gs:
                d = take_bank(("d", f, j)) if g == 0 else live["d", f, j][0]
                nc.tensor.matmul_mx(
                    out=d[:],
                    lhsT=eff_codes[g][:, P * j : P * (j + 1)].bitcast(FP8X4),
                    lhsT_scale=eff_scales[g][:, P * j : P * (j + 1)],
                    rhs=h_codes[f][:, g, :].bitcast(FP8X4),
                    rhs_scale=h_scales[f][:, g, :],
                    start=(g == 0),
                    stop=(g == MACH_GROUPS - 1),
                )

        def hours_operands(f, j):
            live["hours", f, j] = work.tile([P, PACK, P], F32, name="hours", bufs=3)
            return live["hours", f, j][:], empty_bank(("d", f, j))[:].rearrange("p (m t) -> p t m", t=PACK)

        def floor_on_vector(f, j):
            hours, d = hours_operands(f, j)
            nc.vector.tensor_scalar(
                out=hours,
                in0=d,
                scalar1=crew_cols[:, j : j + 1],
                scalar2=crew_cols[:, CREW_TILES + j : CREW_TILES + j + 1],
                op0=ALU.add,
                op1=ALU.max,
            )

        def excess_on_scalar(f, j):
            hours, d = hours_operands(f, j)
            nc.scalar.activation(out=hours, in_=d, func=FUNC.Relu, bias=plan_less_min[:, j : j + 1])

        def floor_on_scalar(f, j):
            excess_on_scalar(f, j)
            hours = live["hours", f, j][:]
            nc.scalar.activation(
                out=hours, in_=hours, func=FUNC.Identity, bias=crew_cols[:, CREW_TILES + j : CREW_TILES + j + 1]
            )

        def turn_hours(f, j):
            bank = take_bank(("hours_turned", f, j))
            for t in range(PACK):
                nc.tensor.transpose(bank[:, P * t : P * (t + 1)], live["hours", f, j][:, t, :], ident[:])

        def lay_minimum(f, j):
            bank = take_bank(("hours_turned", f, j))
            column = crew_cols[:, CREW_TILES + j : CREW_TILES + j + 1].to_broadcast([P, P])
            for t in range(PACK):
                nc.tensor.matmul(
                    bank[:, P * t : P * (t + 1)],
                    lhsT=column,
                    rhs=ident[:],
                    start=(t == 0),
                    stop=False,
                    is_transpose=True,
                )

        def turn_excess(f, j):
            bank = live["hours_turned", f, j][0]
            for t in range(PACK):
                nc.tensor.matmul(
                    bank[:, P * t : P * (t + 1)],
                    lhsT=live["hours", f, j][:, t, :],
                    rhs=ident[:],
                    start=False,
                    stop=(t == PACK - 1),
                    is_transpose=True,
                )

        def finish_y(f, j):
            crews = slice(P * j, P * (j + 1))
            nc.vector.tensor_tensor(
                out=y[f][:, j, :, :],
                in0=empty_bank(("hours_turned", f, j))[:].rearrange("p (t c) -> p t c", t=PACK),
                in1=skill[f][:, :, crews],
                op=ALU.mult,
            )
            nc.sync.dma_start(out=rows_of_group(out_0, f)[:, :, crews], in_=y[f][:, j, :, :])

        def group_y(f, j, copy):
            dst = y_grouped[f][:, P * j : P * (j + 1), :].rearrange("p c t -> p (c t)")
            group_rows(copy, dst, y[f][:, j, :, :])

        def quantize_y(f, j0, j1):
            crews = slice(P * j0, P * j1)
            grouped = y_grouped[f][:, crews, :].rearrange("p c t -> p (c t)")
            quantize(y_codes[f][:, crews], y_scales[f][:, crews], grouped)

        def store_codes(f, j0, j1):
            crews = slice(P * j0, P * j1)
            words = out_1[f].rearrange("p m t -> p (m t)").bitcast(I32)
            nc.sync.dma_start(out=words[:, crews], in_=y_codes[f][:, crews].bitcast(I32))

        def store_scales(f, queues):
            for quad, queue in enumerate(queues):
                queue.dma_start(
                    out=out_2[f, 4 * quad : 4 * quad + 4, :].bitcast(I32),
                    in_=y_scales[f][32 * quad : 32 * quad + 4, :].bitcast(I32),
                )

        nc.vector.memset(warm[:], 0.0)
        nc.gpsimd.memset(crew_rows[:], 0.0)
        make_identity(nc, ident[:])
        nc.gpsimd.memset(expo_rows[:], 0.0)
        nc.scalar.activation(out=warm[:, 1:2], in_=warm[:, 0:1], func=FUNC.Sigmoid)

        load_readings(0, 0, 1)
        load_readings(0, 1, 2)
        load_readings(0, 2, 3)
        load_signatures(0, 0)
        load_signatures(0, 1)
        load_readings(0, 3, 4)
        load_readings(1, 0, 2)
        load_signatures(1, 0)
        load_exposure()
        load_signatures(1, 1)
        load_readings(1, 2, 4)
        load_efforts(0)
        load_efforts(1)
        load_crew_rows(plan, 0)
        load_crew_rows(minimum, CREW_TILES)
        load_readings(2, 0, 2)
        load_efforts(2)
        load_readings(2, 2, 4)
        load_readings(3, 0, 2)
        load_readings(3, 2, 4)
        load_efforts(3)
        load_skills(0)
        load_skills(1)

        turn_readings(0, [0], on_vector)
        quantize_readings(0, 0, 1)
        turn_readings(0, [1])
        quantize_readings(0, 1, 2)
        group_signatures(0, 0, 0, on_scalar)
        turn_readings(0, [2])
        group_signatures(0, 1, 0, on_scalar)
        group_signatures(0, 0, 1, on_vector)
        group_signatures(0, 1, 1, on_vector)
        turn_readings(0, [3])
        turn_readings(1, [0, 1])
        cast_exposure()
        quantize_signatures(0, 0)
        quantize_readings(0, 2, 3)
        quantize_signatures(0, 1)
        quantize_readings(0, 3, 4)
        group_signatures(1, 0, 0, on_vector)
        group_signatures(1, 0, 1, on_vector)
        quantize_readings(1, 0, 2)
        group_signatures(1, 1, 0, on_scalar)
        group_signatures(1, 1, 1, on_vector)
        quantize_signatures(1, 0)
        score(0, 0, [0, 1])
        quantize_signatures(1, 1)
        group_efforts(0, 0, on_vector)
        turn_exposure()
        turn_readings(1, [2, 3])
        score(0, 0, [2, 3])
        group_efforts(0, 1, on_vector)
        quantize_readings(1, 2, 4)
        score(1, 0, [0, 1])
        spill_exposure()
        group_efforts(1, 0, on_vector)

        weigh(0, 0)
        score(0, 1, [0, 1])
        group_efforts(1, 1, on_vector)
        score(1, 0, [2, 3])
        cast_crew_rows()
        quantize_h(0, 0)
        score(0, 1, [2, 3])
        quantize_efforts(0)

        weigh(1, 0)
        turn_readings(2, [0, 1])
        turn_crew_rows()
        quantize_efforts(1)
        quantize_h(1, 0)
        quantize_readings(2, 0, 2)

        weigh(0, 1)
        turn_readings(2, [2, 3])
        score(1, 1)
        group_efforts(2, 0, on_vector)
        turn_readings(3, [0, 1])
        quantize_h(0, 1)
        quantize_readings(2, 2, 4)

        weigh(1, 1)
        quantize_readings(3, 0, 2)
        turn_readings(3, [2, 3])
        score(2, 0, [0, 1])
        quantize_h(1, 1)
        quantize_readings(3, 2, 4)
        score(2, 0, [2, 3])
        score(2, 1, [0, 1])
        score(3, 0, [0, 1])

        weigh(2, 0)
        score(3, 0, [2, 3])
        group_efforts(2, 1, on_vector)
        add_up(0, 1, [0, 1])
        quantize_h(2, 0)
        quantize_efforts(2)
        add_up(0, 0, [0, 1])
        add_up(0, 2, [0, 1])
        group_efforts(3, 0, on_scalar)
        spill_crew_cols()
        group_efforts(3, 1, on_scalar)

        weigh(3, 0)
        score(2, 1, [2, 3])
        add_up(0, 1, [2])
        subtract_minimum()
        quantize_h(3, 0)
        quantize_efforts(3)
        add_up(0, 2, [2])
        add_up(0, 0, [2])

        weigh(2, 1)
        score(3, 1, [0, 1])
        quantize_h(2, 1)
        score(3, 1, [2, 3])
        add_up(0, 0, [3])
        add_up(0, 3, [0, 1, 2])
        add_up(0, 1, [3])
        add_up(0, 3, [3])
        add_up(0, 2, [3])
        floor_on_scalar(0, 0)
        floor_on_vector(0, 1)
        add_up(1, 2, [0, 1, 2])
        turn_hours(0, 0)

        weigh(3, 1)
        finish_y(0, 0)
        floor_on_scalar(0, 2)
        floor_on_scalar(0, 3)
        turn_hours(0, 1)
        quantize_h(3, 1)

        finish_y(0, 1)
        group_y(0, 0, on_scalar)
        add_up(1, 0, [0, 1, 2])
        add_up(1, 1, [0, 1, 2])
        turn_hours(0, 2)
        finish_y(0, 2)
        group_y(0, 1, on_scalar)
        turn_hours(0, 3)
        group_y(0, 2, on_scalar)
        finish_y(0, 3)
        add_up(1, 0, [3])
        group_y(0, 3, on_scalar)
        add_up(1, 1, [3])
        floor_on_vector(1, 0)
        quantize_y(0, 0, 4)
        add_up(1, 3, [0, 1, 2])
        add_up(1, 2, [3])
        add_up(1, 3, [3])
        excess_on_scalar(1, 1)
        turn_hours(1, 0)
        lay_minimum(1, 1)
        turn_excess(1, 1)
        excess_on_scalar(1, 2)
        lay_minimum(1, 2)
        store_codes(0, 0, 4)
        excess_on_scalar(1, 3)
        turn_excess(1, 2)
        store_scales(0, [nc.sync] * 4)
        finish_y(1, 0)
        group_y(1, 0, on_scalar)
        lay_minimum(1, 3)
        finish_y(1, 1)
        turn_excess(1, 3)
        finish_y(1, 2)
        finish_y(1, 3)
        group_y(1, 1, on_scalar)
        quantize_y(1, 0, 2)
        group_y(1, 2, on_scalar)
        group_y(1, 3, on_vector)
        quantize_y(1, 2, 4)
        store_codes(1, 0, 2)
        store_codes(1, 2, 4)
        store_scales(1, [nc.sync, nc.sync, nc.scalar, nc.scalar])
